import numpy as np
import ml_dtypes


def mxq(x, axis, fmt="e4m3"):
    dtype, down = {"e4m3": (ml_dtypes.float8_e4m3fn, 7), "e5m2": (ml_dtypes.float8_e5m2, 14)}[fmt]
    v = np.moveaxis(np.asarray(x, np.float32).astype(ml_dtypes.bfloat16).astype(np.float64), axis, -1)
    blocks = v.reshape(v.shape[:-1] + (-1, 32))
    amax = np.abs(blocks).max(-1, keepdims=True)
    byte = np.maximum(np.where(amax > 0, np.frexp(amax)[1] - 1 + 127, 0) - down, 1)
    scale = np.exp2(byte - 127.0)
    codes = (blocks / scale).astype(np.float32).astype(dtype).astype(np.float64)
    return np.moveaxis((codes * scale).reshape(v.shape), -1, axis)


WIDE = False


def mx_kscale(k):
    if not WIDE:
        return np.ones(k)
    levels = np.array([10, -10, 5, -5, 0])
    if k % 512:
        return np.exp2(np.random.permutation(np.resize(levels, k // 32))).repeat(32)
    a = np.empty((k // 512, 16))
    for p in range(k // 512):
        a[p, :8] = np.random.permutation(np.resize(levels, 8))
        for g in range(8):
            far = levels[np.abs(levels - a[p, g]) >= 10]
            a[p, g + 8] = far[np.random.randint(len(far))]
    return np.exp2(a.ravel()).repeat(32)


def f64(x):
    return np.asarray(x).astype(np.float64)


def striped(idx):
    return np.tile(idx.reshape(-1, 16).T, (8, 1)).astype(np.uint16)


def unstriped(offs):
    return offs[:16].T.reshape(-1).astype(np.int64)


def silu(v):
    return v / (1.0 + np.exp(-np.maximum(v, -700.0)))


K, T, E, C, N = 2048, 1024, 2, 256, 128


def by_expert(wq, xq):
    return np.concatenate([wq[e].T @ xq[:, e * C:(e + 1) * C] for e in range(E)], axis=1)


def setup_inputs():
    n = np.random.standard_normal
    s = mx_kscale(K)[:, None]
    return {
        "xT": (n((K, T)) * s).astype(np.float32),
        "w": (n((E + 1, K, N)) / np.sqrt(K) / s[None]).astype(np.float32),
        "b": (0.3 * n((N, E + 1))).astype(np.float32),
        "gate": np.tile(np.random.uniform(0.2, 1.0, E * C), (N, 1)).astype(np.float32),
        "offs": striped(np.random.permutation(T)[:E * C]),
    }


def reference(xT, w, b, gate, offs):
    idx = unstriped(offs)
    wq = mxq(f64(w), 1, "e4m3")
    xs = mxq(f64(xT), 0, "e4m3")
    ys = silu((wq[E].T @ xs) + f64(b)[:, E:])
    xq = mxq(f64(xT)[:, idx], 0, "e4m3")
    y = by_expert(wq, xq)
    y = silu(y + np.repeat(f64(b)[:, :E], C, axis=1))
    out = ys
    out[:, idx] += f64(gate) * y
    return out

@@ -1,0 +1,260 @@
+from contextlib import ExitStack
+
+import concourse.mybir as mybir
+
+K, T, E, C, N = 2048, 1024, 2, 256, 128
+S = E * C
+P = 128
+PASSES = K // 512
+FLOPS = 2 * K * N * (T + S)
+
+F32 = mybir.dt.float32
+BF16 = mybir.dt.bfloat16
+U32 = mybir.dt.uint32
+U16 = mybir.dt.uint16
+U8 = mybir.dt.uint8
+FP8X4 = mybir.dt.float8_e4m3fn_x4
+SILU = mybir.ActivationFunctionType.Silu
+MULT = mybir.AluOpType.mult
+ADD = mybir.AluOpType.add
+
+
+def tile_moe_shr_lin_silu_kernel(tc, xT, w, b, gate, offs, out):
+    nc = tc.nc
+    with ExitStack() as ctx:
+        keep = ctx.enter_context(tc.tile_pool(name="keep", bufs=1))
+        ring = ctx.enter_context(tc.tile_pool(name="ring", bufs=3))
+        late = ctx.enter_context(tc.tile_pool(name="late", bufs=1))
+        psum = ctx.enter_context(tc.psum_pool(name="psum", bufs=1))
+
+        offsets = keep.tile([P, S // 16], U16, name="offsets")
+        bias = keep.tile([P, E + 1], F32, name="bias")
+        gates = keep.tile([P, S], F32, name="gates")
+        scattered = keep.tile([P, T], F32, name="scattered")
+        warm = keep.tile([P, 1], F32, name="warm")
+
+        nc.gpsimd.memset(warm[:], 0.0)
+        nc.scalar.activation(warm[:], warm[:], SILU)
+        nc.gpsimd.memset(scattered[:], 0.0)
+
+        x_raw = [[keep.tile([P, 2 * T], F32, name="x_raw_%d_%d" % (c, u)) for u in range(2)] for c in range(PASSES)]
+        wr_raw = [keep.tile([P, 4 * 4 * N], F32, name="wr_raw_%d" % h) for h in range(2)]
+        ws_raw = [keep.tile([P, 2 * 4 * N], F32, name="ws_raw_%d" % h) for h in range(2)]
+
+        def load_x(c, u, half=None):
+            rows = xT[c * 512:(c + 1) * 512, :].rearrange("(p j) t -> p j t", j=4)
+            lo, step = (0, T) if half is None else (half * 512, 512)
+            dst = x_raw[c][u][:, 2 * lo:2 * (lo + step)].rearrange("p (j t) -> p j t", j=2)
+            nc.sync.dma_start(out=dst, in_=rows[:, 2 * u:2 * u + 2, lo:lo + step])
+
+        def load_w(dst, e, c0, passes):
+            nc.sync.dma_start(
+                out=dst.rearrange("p (c r) -> p c r", c=passes),
+                in_=w[e, c0 * 512:(c0 + passes) * 512, :].rearrange("(c p j) n -> p c (j n)", p=P, j=4),
+            )
+
+        load_x(0, 0, 0)
+        load_x(0, 1, 0)
+        nc.sync.dma_start(offsets[:], offs)
+        nc.scalar.dma_start(out=bias[:], in_=b)
+        load_x(0, 0, 1)
+        load_x(0, 1, 1)
+        for c in range(1, 3):
+         for u in range(2):
+             load_x(c, u)
+        for h in range(2):
+         load_x(3, h)
+         for e in range(2):
+             load_w(wr_raw[h][:, e * 1024:(e + 1) * 1024], e, 2 * h, 2)
+        load_w(ws_raw[0][:], 2, 0, 2)
+        nc.sync.dma_start(gates[:], gate)
+        load_w(ws_raw[1][:], 2, 2, 2)
+
+        acc_r = [psum.tile([P, C], F32, name="acc_r_%d" % e) for e in range(E)]
+        acc_s = [psum.tile([P, 512], F32, name="acc_s_%d" % h) for h in range(2)]
+        xs_codes = [keep.tile([P, T], U32, name="xs_codes_%d" % c, align_bytes=64) for c in range(PASSES)]
+        xs_scales = [keep.tile([P, T], U8, name="xs_scales_%d" % c, align_bytes=64) for c in range(PASSES)]
+        xr_codes = [keep.tile([P, S], U32, name="xr_codes_%d" % c, align_bytes=64) for c in range(PASSES)]
+        xr_scales = [keep.tile([P, S], U8, name="xr_scales_%d" % c, align_bytes=64) for c in range(PASSES)]
+        w_codes = [keep.tile([P, 512 if i < 2 else 256], U32, name="w_codes_%d" % i, align_bytes=64) for i in range(4)]
+        w_scales = [keep.tile([P, 512 if i < 2 else 256], U8, name="w_scales_%d" % i, align_bytes=64) for i in range(4)]
+        pp = [ring.tile([P, 4096], BF16, name="pp", align_bytes=64) for c in range(PASSES)]
+        g = [ring.tile([P, 2048], BF16, name="g", align_bytes=64) for c in range(PASSES)]
+        xs = [ring.tile([P, 4096], BF16, name="xs", align_bytes=64) for c in range(PASSES)]
+        late_w = late.tile([P, 2048], BF16, name="late_w", tag="late", align_bytes=64)
+        late_xs = late.tile([P, 2048], BF16, name="late_xs", tag="late", align_bytes=64)
+        xr = [ring.tile([P, 2048], BF16, name="xr", align_bytes=64) for c in range(PASSES)]
+
+        def planes(c, u, engines=(nc.scalar.copy,)):
+            step = T // len(engines)
+            for i, copy in enumerate(engines):
+                if copy is None:
+                    continue
+                src = x_raw[c][u][:, i * 2 * step:(i + 1) * 2 * step].rearrange("p (j t) -> p t j", j=2)
+                lo = u * 2048 + i * 2 * step
+                copy(pp[c][:, lo:lo + 2 * step].rearrange("p (t j) -> p t j", j=2), src)
+
+        def group_w(raw, blocks, grouped=None):
+            if grouped is None:
+                grouped = ring.tile([P, 512 * blocks], BF16, name="w_grouped", align_bytes=64)
+            nc.scalar.copy(
+                grouped[:].rearrange("p (q n j) -> p q n j", q=blocks, j=4),
+                raw[:].rearrange("p (q j n) -> p q n j", q=blocks, j=4),
+            )
+            return grouped
+
+        def quant_w(i, grouped):
+            nc.vector.quantize_mx(out=w_codes[i][:].bitcast(FP8X4), scales=w_scales[i][:], in_=grouped[:])
+
+        def gather(c, u):
+            nc.vector.tensor_copy(
+                g[c][:, u * 1024:(u + 1) * 1024].bitcast(U32),
+                pp[c][:, u * 2048:(u + 1) * 2048].bitcast(U32).indirect(offsets[:]),
+            )
+
+        def inter_s(c, lo=0, hi=T, copy=nc.vector.tensor_copy):
+            copy(
+                xs[c][:].bitcast(F32).rearrange("p (t u) -> p t u", u=2)[:, lo:hi],
+                pp[c][:].bitcast(F32).rearrange("p (u t) -> p t u", u=2)[:, lo:hi],
+            )
+
+        def inter_late():
+            nc.vector.tensor_copy(
+                late_xs[:].bitcast(F32).rearrange("p (t u) -> p t u", u=2),
+                pp[3][:].bitcast(F32).rearrange("p (u t) -> p t u", u=2)[:, 512:],
+            )
+
+        def quant_late():
+            s = slice(512, T)
+            nc.vector.quantize_mx(out=xs_codes[3][:, s].bitcast(FP8X4), scales=xs_scales[3][:, s], in_=late_xs[:])
+
+        def inter_g(c, copy=nc.vector.tensor_copy):
+            copy(
+                xr[c][:].bitcast(F32).rearrange("p (t u) -> p t u", u=2),
+                g[c][:].bitcast(F32).rearrange("p (u t) -> p t u", u=2),
+            )
+
+        def quant_r(c):
+            nc.vector.quantize_mx(out=xr_codes[c][:].bitcast(FP8X4), scales=xr_scales[c][:], in_=xr[c][:])
+
+        def quant_s(c, lo=0, hi=T):
+            nc.vector.quantize_mx(
+                out=xs_codes[c][:, lo:hi].bitcast(FP8X4), scales=xs_scales[c][:, lo:hi], in_=xs[c][:, 4 * lo:4 * hi])
+
+        def routed(c):
+            i, k = c // 2, c % 2
+            for e in range(E):
+                q = slice((e * 2 + k) * N, (e * 2 + k + 1) * N)
+                s = slice(e * C, (e + 1) * C)
+                nc.tensor.matmul_mx(
+                    out=acc_r[e][:], lhsT=w_codes[i][:, q].bitcast(FP8X4), lhsT_scale=w_scales[i][:, q],
+                    rhs=xr_codes[c][:, s].bitcast(FP8X4), rhs_scale=xr_scales[c][:, s],
+                    start=(c == 0), stop=(c == PASSES - 1),
+                )
+
+        def shared(c, h):
+            i, k = 2 + c // 2, c % 2
+            q = slice(k * N, (k + 1) * N)
+            s = slice(h * 512, (h + 1) * 512)
+            nc.tensor.matmul_mx(
+                out=acc_s[h][:], lhsT=w_codes[i][:, q].bitcast(FP8X4), lhsT_scale=w_scales[i][:, q],
+                rhs=xs_codes[c][:, s].bitcast(FP8X4), rhs_scale=xs_scales[c][:, s],
+                start=(c == 0), stop=(c == PASSES - 1),
+            )
+
+        y = keep.tile([P, S], F32, name="y")
+        ys = keep.tile([P, T], F32, name="ys")
+
+        def act_r(e):
+            s = slice(e * C, (e + 1) * C)
+            nc.scalar.activation(y[:, s], acc_r[e][:], SILU, bias=bias[:, e:e + 1])
+
+        def scatter(e):
+            s = slice(e * C, (e + 1) * C)
+            nc.vector.tensor_tensor(
+                scattered[:].indirect(offsets[:, e * 16:(e + 1) * 16]), y[:, s], gates[:, s], MULT)
+
+        gy = keep.tile([P, S], F32, name="gy")
+
+        def scatter_all():
+            nc.vector.tensor_tensor(scattered[:].indirect(offsets[:]), y[:], gates[:], MULT)
+
+        def gate_mul(e, eng=nc.gpsimd):
+            s = slice(e * C, (e + 1) * C)
+            eng.tensor_tensor(gy[:, s], y[:, s], gates[:, s], MULT)
+
+        def scatter_copy(e):
+            s = slice(e * C, (e + 1) * C)
+            nc.vector.tensor_copy(scattered[:].indirect(offsets[:, e * 16:(e + 1) * 16]), gy[:, s])
+
+        def act_s(lo, hi):
+            h = lo // 512
+            nc.scalar.activation(ys[:, lo:hi], acc_s[h][:, lo - 512 * h:hi - 512 * h], SILU, bias=bias[:, E:E + 1])
+
+        res = keep.tile([P, T], F32, name="res")
+
+        def finish(lo, hi):
+            nc.vector.tensor_tensor(res[:, lo:hi], ys[:, lo:hi], scattered[:, lo:hi], ADD)
+            nc.sync.dma_start(out=out[:, lo:hi], in_=res[:, lo:hi])
+
+        cs, cv = nc.scalar.copy, nc.vector.tensor_copy
+        planes(0, 0, (cs, None))
+        planes(0, 1, (cv, None))
+        inter_s(0, 0, 512)
+        planes(0, 0, (None, cs))
+        quant_s(0, 0, 512)
+        gather(0, 0)
+        planes(0, 1, (None, cs))
+        gather(0, 1)
+        planes(1, 0)
+        inter_s(0, 512, 1024)
+        inter_g(0)
+        quant_s(0, 512, 1024)
+        quant_r(0)
+        planes(1, 1)
+        planes(2, 0)
+        gather(1, 0)
+        planes(2, 1)
+        gather(1, 1)
+        inter_s(1)
+        inter_g(1)
+        quant_s(1)
+        quant_r(1)
+        planes(3, 0)
+        gather(2, 0)
+        gather(2, 1)
+        inter_s(2)
+        wg0 = group_w(wr_raw[0], 4)
+        inter_g(2)
+        quant_s(2)
+        planes(3, 1)
+        gather(3, 0)
+        quant_w(0, wg0)
+        quant_r(2)
+        routed(0)
+        routed(1)
+        wg1 = group_w(wr_raw[1], 4, late_w)
+        gather(3, 1)
+        inter_s(3, 0, 512)
+        inter_g(3)
+        quant_s(3, 0, 512)
+        quant_r(3)
+        quant_w(1, wg1)
+        routed(2)
+        routed(3)
+        inter_late()
+        wg2 = group_w(ws_raw[0], 2)
+        wg3 = group_w(ws_raw[1], 2)
+        for e in range(2):
+         act_r(e)
+        quant_w(2, wg2)
+        quant_late()
+        quant_w(3, wg3)
+        for c in range(PASSES):
+         for h in range(2):
+             shared(c, h)
+        scatter_all()
+        for h in range(2):
+         act_s(h * 512, h * 512 + 512)
+        for h in range(2):
+         finish(h * 512, h * 512 + 512)

@@ -98,8 +98,8 @@ def tile_moe_shr_lin_silu_kernel(tc, xT, w, b, gate, offs, out):
             if grouped is None:
                 grouped = ring.tile([P, 512 * blocks], BF16, name="w_grouped", align_bytes=64)
             nc.scalar.copy(
-                grouped[:].rearrange("p (q n j) -> p q n j", q=blocks, j=4),
-                raw[:].rearrange("p (q j n) -> p q n j", q=blocks, j=4),
+                grouped[:].rearrange("p (q c i j) -> p q c j i", q=blocks, i=4, j=4),
+                raw[:].rearrange("p (q j c i) -> p q c j i", q=blocks, i=4, j=4),
             )
             return grouped
 

@@ -24,7 +24,6 @@ def tile_moe_shr_lin_silu_kernel(tc, xT, w, b, gate, offs, out):
     with ExitStack() as ctx:
         keep = ctx.enter_context(tc.tile_pool(name="keep", bufs=1))
         ring = ctx.enter_context(tc.tile_pool(name="ring", bufs=3))
-        late = ctx.enter_context(tc.tile_pool(name="late", bufs=1))
         psum = ctx.enter_context(tc.psum_pool(name="psum", bufs=1))
 
         offsets = keep.tile([P, S // 16], U16, name="offsets")
@@ -38,20 +37,25 @@ def tile_moe_shr_lin_silu_kernel(tc, xT, w, b, gate, offs, out):
         nc.gpsimd.memset(scattered[:], 0.0)
 
         x_raw = [[keep.tile([P, 2 * T], F32, name="x_raw_%d_%d" % (c, u)) for u in range(2)] for c in range(PASSES)]
-        wr_raw = [keep.tile([P, 4 * 4 * N], F32, name="wr_raw_%d" % h) for h in range(2)]
-        ws_raw = [keep.tile([P, 2 * 4 * N], F32, name="ws_raw_%d" % h) for h in range(2)]
+        blocks = [(c, e) for c in range(2) for e in range(3)] + [(c, e) for c in range(2, 4) for e in range(2)] + [(2, 2), (3, 2)]
+        w_raw = keep.tile([P, 12 * 512], F32, name="w_raw")
+        halved = {}
 
         def load_x(c, u, half=None):
             rows = xT[c * 512:(c + 1) * 512, :].rearrange("(p j) t -> p j t", j=4)
             lo, step = (0, T) if half is None else (half * 512, 512)
+            halved[(c, u)] = half is not None
             dst = x_raw[c][u][:, 2 * lo:2 * (lo + step)].rearrange("p (j t) -> p j t", j=2)
             nc.sync.dma_start(out=dst, in_=rows[:, 2 * u:2 * u + 2, lo:lo + step])
 
-        def load_w(dst, e, c0, passes):
-            nc.sync.dma_start(
-                out=dst.rearrange("p (c r) -> p c r", c=passes),
-                in_=w[e, c0 * 512:(c0 + passes) * 512, :].rearrange("(c p j) n -> p c (j n)", p=P, j=4),
-            )
+        def load_w(q0, q1):
+            (c0, e0), (c1, e1) = blocks[q0], blocks[q1 - 1]
+            dst = w_raw[:, q0 * 512:q1 * 512].rearrange("p (q r) -> p q r", q=q1 - q0)
+            if c0 == c1:
+                src = w[e0:e1 + 1, c0 * 512:(c0 + 1) * 512, :].rearrange("e (p j) n -> p e (j n)", j=4)
+            else:
+                src = w[e0, c0 * 512:(c1 + 1) * 512, :].rearrange("(c p j) n -> p c (j n)", p=P, j=4)
+            nc.sync.dma_start(out=dst, in_=src)
 
         load_x(0, 0, 0)
         load_x(0, 1, 0)
@@ -59,16 +63,19 @@ def tile_moe_shr_lin_silu_kernel(tc, xT, w, b, gate, offs, out):
         nc.scalar.dma_start(out=bias[:], in_=b)
         load_x(0, 0, 1)
         load_x(0, 1, 1)
-        for c in range(1, 3):
-         for u in range(2):
-             load_x(c, u)
-        for h in range(2):
-         load_x(3, h)
-         for e in range(2):
-             load_w(wr_raw[h][:, e * 1024:(e + 1) * 1024], e, 2 * h, 2)
-        load_w(ws_raw[0][:], 2, 0, 2)
+        for u in range(2):
+            for h in range(2):
+                load_x(1, u, h)
+        load_w(0, 3)
+        load_x(2, 0)
+        load_x(2, 1)
+        load_w(3, 6)
+        load_x(3, 0)
+        load_w(6, 8)
+        load_x(3, 1)
+        load_w(8, 10)
+        load_w(10, 12)
         nc.sync.dma_start(gates[:], gate)
-        load_w(ws_raw[1][:], 2, 2, 2)
 
         acc_r = [psum.tile([P, C], F32, name="acc_r_%d" % e) for e in range(E)]
         acc_s = [psum.tile([P, 512], F32, name="acc_s_%d" % h) for h in range(2)]
@@ -76,35 +83,31 @@ def tile_moe_shr_lin_silu_kernel(tc, xT, w, b, gate, offs, out):
         xs_scales = [keep.tile([P, T], U8, name="xs_scales_%d" % c, align_bytes=64) for c in range(PASSES)]
         xr_codes = [keep.tile([P, S], U32, name="xr_codes_%d" % c, align_bytes=64) for c in range(PASSES)]
         xr_scales = [keep.tile([P, S], U8, name="xr_scales_%d" % c, align_bytes=64) for c in range(PASSES)]
-        w_codes = [keep.tile([P, 512 if i < 2 else 256], U32, name="w_codes_%d" % i, align_bytes=64) for i in range(4)]
-        w_scales = [keep.tile([P, 512 if i < 2 else 256], U8, name="w_scales_%d" % i, align_bytes=64) for i in range(4)]
+        w_bf = keep.tile([P, 12 * 512], BF16, name="w_bf", align_bytes=64)
+        w_codes = keep.tile([P, 12 * N], U32, name="w_codes", align_bytes=64)
+        w_scales = keep.tile([P, 12 * N], U8, name="w_scales", align_bytes=64)
         pp = [ring.tile([P, 4096], BF16, name="pp", align_bytes=64) for c in range(PASSES)]
         g = [ring.tile([P, 2048], BF16, name="g", align_bytes=64) for c in range(PASSES)]
         xs = [ring.tile([P, 4096], BF16, name="xs", align_bytes=64) for c in range(PASSES)]
-        late_w = late.tile([P, 2048], BF16, name="late_w", tag="late", align_bytes=64)
-        late_xs = late.tile([P, 2048], BF16, name="late_xs", tag="late", align_bytes=64)
         xr = [ring.tile([P, 2048], BF16, name="xr", align_bytes=64) for c in range(PASSES)]
 
-        def planes(c, u, engines=(nc.scalar.copy,)):
-            step = T // len(engines)
-            for i, copy in enumerate(engines):
-                if copy is None:
-                    continue
-                src = x_raw[c][u][:, i * 2 * step:(i + 1) * 2 * step].rearrange("p (j t) -> p t j", j=2)
-                lo = u * 2048 + i * 2 * step
-                copy(pp[c][:, lo:lo + 2 * step].rearrange("p (t j) -> p t j", j=2), src)
 
-        def group_w(raw, blocks, grouped=None):
-            if grouped is None:
-                grouped = ring.tile([P, 512 * blocks], BF16, name="w_grouped", align_bytes=64)
-            nc.scalar.copy(
-                grouped[:].rearrange("p (q c i j) -> p q c j i", q=blocks, i=4, j=4),
-                raw[:].rearrange("p (q j c i) -> p q c j i", q=blocks, i=4, j=4),
+        def planes(c, u, lo=0, hi=T, copy=nc.scalar.copy):
+            step = 512 if halved[(c, u)] else T
+            base = lo // step * step
+            piece = x_raw[c][u][:, 2 * base:2 * (base + step)].rearrange("p (j t) -> p t j", j=2)
+            dst = pp[c][:, u * 2048 + 2 * lo:u * 2048 + 2 * hi].rearrange("p (t j) -> p t j", j=2)
+            copy(dst, piece[:, lo - base:hi - base])
+
+        def group_w(q0, q1, copy=nc.scalar.copy):
+            copy(
+                w_bf[:, q0 * 512:q1 * 512].rearrange("p (q c i j) -> p q c j i", q=q1 - q0, i=4, j=4),
+                w_raw[:, q0 * 512:q1 * 512].rearrange("p (q j c i) -> p q c j i", q=q1 - q0, i=4, j=4),
             )
-            return grouped
 
-        def quant_w(i, grouped):
-            nc.vector.quantize_mx(out=w_codes[i][:].bitcast(FP8X4), scales=w_scales[i][:], in_=grouped[:])
+        def quant_w(q0, q1):
+            s = slice(q0 * N, q1 * N)
+            nc.vector.quantize_mx(out=w_codes[:, s].bitcast(FP8X4), scales=w_scales[:, s], in_=w_bf[:, q0 * 512:q1 * 512])
 
         def gather(c, u):
             nc.vector.tensor_copy(
@@ -112,21 +115,11 @@ def tile_moe_shr_lin_silu_kernel(tc, xT, w, b, gate, offs, out):
                 pp[c][:, u * 2048:(u + 1) * 2048].bitcast(U32).indirect(offsets[:]),
             )
 
-        def inter_s(c, lo=0, hi=T, copy=nc.vector.tensor_copy):
+        def inter_s(c, lo=0, hi=T, copy=nc.vector.tensor_copy, dt=F32):
             copy(
-                xs[c][:].bitcast(F32).rearrange("p (t u) -> p t u", u=2)[:, lo:hi],
-                pp[c][:].bitcast(F32).rearrange("p (u t) -> p t u", u=2)[:, lo:hi],
+                xs[c][:].bitcast(dt).rearrange("p (t u) -> p t u", u=2)[:, lo:hi],
+                pp[c][:].bitcast(dt).rearrange("p (u t) -> p t u", u=2)[:, lo:hi],
             )
-
-        def inter_late():
-            nc.vector.tensor_copy(
-                late_xs[:].bitcast(F32).rearrange("p (t u) -> p t u", u=2),
-                pp[3][:].bitcast(F32).rearrange("p (u t) -> p t u", u=2)[:, 512:],
-            )
-
-        def quant_late():
-            s = slice(512, T)
-            nc.vector.quantize_mx(out=xs_codes[3][:, s].bitcast(FP8X4), scales=xs_scales[3][:, s], in_=late_xs[:])
 
         def inter_g(c, copy=nc.vector.tensor_copy):
             copy(
@@ -142,119 +135,106 @@ def tile_moe_shr_lin_silu_kernel(tc, xT, w, b, gate, offs, out):
                 out=xs_codes[c][:, lo:hi].bitcast(FP8X4), scales=xs_scales[c][:, lo:hi], in_=xs[c][:, 4 * lo:4 * hi])
 
         def routed(c):
-            i, k = c // 2, c % 2
             for e in range(E):
-                q = slice((e * 2 + k) * N, (e * 2 + k + 1) * N)
+                q = slice(blocks.index((c, e)) * N, (blocks.index((c, e)) + 1) * N)
                 s = slice(e * C, (e + 1) * C)
                 nc.tensor.matmul_mx(
-                    out=acc_r[e][:], lhsT=w_codes[i][:, q].bitcast(FP8X4), lhsT_scale=w_scales[i][:, q],
+                    out=acc_r[e][:], lhsT=w_codes[:, q].bitcast(FP8X4), lhsT_scale=w_scales[:, q],
                     rhs=xr_codes[c][:, s].bitcast(FP8X4), rhs_scale=xr_scales[c][:, s],
                     start=(c == 0), stop=(c == PASSES - 1),
                 )
 
         def shared(c, h):
-            i, k = 2 + c // 2, c % 2
-            q = slice(k * N, (k + 1) * N)
+            q = slice(blocks.index((c, E)) * N, (blocks.index((c, E)) + 1) * N)
             s = slice(h * 512, (h + 1) * 512)
             nc.tensor.matmul_mx(
-                out=acc_s[h][:], lhsT=w_codes[i][:, q].bitcast(FP8X4), lhsT_scale=w_scales[i][:, q],
+                out=acc_s[h][:], lhsT=w_codes[:, q].bitcast(FP8X4), lhsT_scale=w_scales[:, q],
                 rhs=xs_codes[c][:, s].bitcast(FP8X4), rhs_scale=xs_scales[c][:, s],
                 start=(c == 0), stop=(c == PASSES - 1),
             )
 
         y = keep.tile([P, S], F32, name="y")
         ys = keep.tile([P, T], F32, name="ys")
+        res = keep.tile([P, T], F32, name="res")
 
         def act_r(e):
             s = slice(e * C, (e + 1) * C)
             nc.scalar.activation(y[:, s], acc_r[e][:], SILU, bias=bias[:, e:e + 1])
 
-        def scatter(e):
-            s = slice(e * C, (e + 1) * C)
-            nc.vector.tensor_tensor(
-                scattered[:].indirect(offsets[:, e * 16:(e + 1) * 16]), y[:, s], gates[:, s], MULT)
-
-        gy = keep.tile([P, S], F32, name="gy")
-
         def scatter_all():
             nc.vector.tensor_tensor(scattered[:].indirect(offsets[:]), y[:], gates[:], MULT)
 
-        def gate_mul(e, eng=nc.gpsimd):
-            s = slice(e * C, (e + 1) * C)
-            eng.tensor_tensor(gy[:, s], y[:, s], gates[:, s], MULT)
+        def act_s(h):
+            nc.scalar.activation(ys[:, h * 512:(h + 1) * 512], acc_s[h][:], SILU, bias=bias[:, E:E + 1])
 
-        def scatter_copy(e):
-            s = slice(e * C, (e + 1) * C)
-            nc.vector.tensor_copy(scattered[:].indirect(offsets[:, e * 16:(e + 1) * 16]), gy[:, s])
-
-        def act_s(lo, hi):
-            h = lo // 512
-            nc.scalar.activation(ys[:, lo:hi], acc_s[h][:, lo - 512 * h:hi - 512 * h], SILU, bias=bias[:, E:E + 1])
-
-        res = keep.tile([P, T], F32, name="res")
-
-        def finish(lo, hi):
+        def finish(lo, hi, queue=nc.sync):
             nc.vector.tensor_tensor(res[:, lo:hi], ys[:, lo:hi], scattered[:, lo:hi], ADD)
-            nc.sync.dma_start(out=out[:, lo:hi], in_=res[:, lo:hi])
+            queue.dma_start(out=out[:, lo:hi], in_=res[:, lo:hi])
 
         cs, cv = nc.scalar.copy, nc.vector.tensor_copy
-        planes(0, 0, (cs, None))
-        planes(0, 1, (cv, None))
+        planes(0, 0, 0, 512)
+        planes(0, 1, 0, 512, cv)
         inter_s(0, 0, 512)
-        planes(0, 0, (None, cs))
+        planes(0, 0, 512, T)
         quant_s(0, 0, 512)
         gather(0, 0)
-        planes(0, 1, (None, cs))
+        planes(0, 1, 512, T)
         gather(0, 1)
-        planes(1, 0)
-        inter_s(0, 512, 1024)
+        for u in range(2):
+            for h in range(2):
+                planes(1, u, h * 512, h * 512 + 512)
+        inter_s(0, 512, T)
         inter_g(0)
-        quant_s(0, 512, 1024)
+        quant_s(0, 512, T)
         quant_r(0)
-        planes(1, 1)
-        planes(2, 0)
         gather(1, 0)
-        planes(2, 1)
         gather(1, 1)
+        group_w(0, 3)
         inter_s(1)
         inter_g(1)
+        planes(2, 0)
+        planes(2, 1)
         quant_s(1)
         quant_r(1)
-        planes(3, 0)
         gather(2, 0)
         gather(2, 1)
+        group_w(3, 6)
         inter_s(2)
-        wg0 = group_w(wr_raw[0], 4)
         inter_g(2)
-        quant_s(2)
+        planes(3, 0)
+        group_w(6, 8)
         planes(3, 1)
-        gather(3, 0)
-        quant_w(0, wg0)
+        quant_s(2)
         quant_r(2)
+        quant_w(0, 4)
         routed(0)
+        shared(0, 0)
+        shared(0, 1)
+        gather(3, 0)
+        quant_w(4, 8)
         routed(1)
-        wg1 = group_w(wr_raw[1], 4, late_w)
-        gather(3, 1)
-        inter_s(3, 0, 512)
-        inter_g(3)
-        quant_s(3, 0, 512)
-        quant_r(3)
-        quant_w(1, wg1)
         routed(2)
+        shared(1, 0)
+        shared(1, 1)
+        gather(3, 1)
+        group_w(8, 10)
+        inter_g(3)
+        quant_w(8, 10)
+        quant_r(3)
         routed(3)
-        inter_late()
-        wg2 = group_w(ws_raw[0], 2)
-        wg3 = group_w(ws_raw[1], 2)
-        for e in range(2):
-         act_r(e)
-        quant_w(2, wg2)
-        quant_late()
-        quant_w(3, wg3)
-        for c in range(PASSES):
-         for h in range(2):
-             shared(c, h)
+        inter_s(3, 0, 512, cs)
+        inter_s(3, 512, T, cs)
+        group_w(10, 12)
+        act_r(0)
+        act_r(1)
+        quant_s(3, 0, 512)
+        quant_s(3, 512, T)
+        quant_w(10, 12)
+        for h in range(2):
+            for c in range(2, 4):
+                shared(c, h)
         scatter_all()
         for h in range(2):
-         act_s(h * 512, h * 512 + 512)
+            act_s(h)
         for h in range(2):
-         finish(h * 512, h * 512 + 512)
+            finish(h * 512, h * 512 + 512)

@@ -37,7 +37,7 @@ def tile_moe_shr_lin_silu_kernel(tc, xT, w, b, gate, offs, out):
         nc.gpsimd.memset(scattered[:], 0.0)
 
         x_raw = [[keep.tile([P, 2 * T], F32, name="x_raw_%d_%d" % (c, u)) for u in range(2)] for c in range(PASSES)]
-        blocks = [(c, e) for c in range(2) for e in range(3)] + [(c, e) for c in range(2, 4) for e in range(2)] + [(2, 2), (3, 2)]
+        blocks = [(c, e) for c in range(4) for e in range(2)] + [(c, 2) for c in range(4)]
         w_raw = keep.tile([P, 12 * 512], F32, name="w_raw")
         halved = {}
 
@@ -66,13 +66,14 @@ def tile_moe_shr_lin_silu_kernel(tc, xT, w, b, gate, offs, out):
         for u in range(2):
             for h in range(2):
                 load_x(1, u, h)
-        load_w(0, 3)
         load_x(2, 0)
         load_x(2, 1)
-        load_w(3, 6)
+        load_w(0, 2)
+        load_w(2, 4)
         load_x(3, 0)
-        load_w(6, 8)
         load_x(3, 1)
+        load_w(4, 6)
+        load_w(6, 8)
         load_w(8, 10)
         load_w(10, 12)
         nc.sync.dma_start(gates[:], gate)
@@ -189,8 +190,8 @@ def tile_moe_shr_lin_silu_kernel(tc, xT, w, b, gate, offs, out):
         quant_r(0)
         gather(1, 0)
         gather(1, 1)
-        group_w(0, 3)
-        inter_s(1)
+        inter_s(1, 0, 512, cs)
+        inter_s(1, 512, T)
         inter_g(1)
         planes(2, 0)
         planes(2, 1)
@@ -198,35 +199,35 @@ def tile_moe_shr_lin_silu_kernel(tc, xT, w, b, gate, offs, out):
         quant_r(1)
         gather(2, 0)
         gather(2, 1)
-        group_w(3, 6)
         inter_s(2)
         inter_g(2)
+        group_w(0, 4)
         planes(3, 0)
-        group_w(6, 8)
         planes(3, 1)
         quant_s(2)
         quant_r(2)
+        gather(3, 0)
         quant_w(0, 4)
         routed(0)
-        shared(0, 0)
-        shared(0, 1)
-        gather(3, 0)
-        quant_w(4, 8)
         routed(1)
-        routed(2)
-        shared(1, 0)
-        shared(1, 1)
         gather(3, 1)
+        group_w(4, 6)
+        group_w(6, 8)
         group_w(8, 10)
-        inter_g(3)
-        quant_w(8, 10)
-        quant_r(3)
-        routed(3)
-        inter_s(3, 0, 512, cs)
-        inter_s(3, 512, T, cs)
         group_w(10, 12)
+        inter_s(3, 0, 512)
+        inter_g(3)
+        inter_s(3, 512, T)
+        quant_r(3)
+        quant_w(4, 8)
+        routed(2)
+        routed(3)
         act_r(0)
         act_r(1)
+        quant_w(8, 10)
+        for h in range(2):
+            for c in range(2):
+                shared(c, h)
         quant_s(3, 0, 512)
         quant_s(3, 512, T)
         quant_w(10, 12)

@@ -38,7 +38,7 @@ def tile_moe_shr_lin_silu_kernel(tc, xT, w, b, gate, offs, out):
 
         x_raw = [[keep.tile([P, 2 * T], F32, name="x_raw_%d_%d" % (c, u)) for u in range(2)] for c in range(PASSES)]
         blocks = [(c, e) for c in range(4) for e in range(2)] + [(c, 2) for c in range(4)]
-        w_raw = keep.tile([P, 12 * 512], F32, name="w_raw")
+        w_raw = keep.tile([P, 12 * 512], F32, name="w_raw", align_bytes=64)
         halved = {}
 
         def load_x(c, u, half=None):
@@ -69,9 +69,10 @@ def tile_moe_shr_lin_silu_kernel(tc, xT, w, b, gate, offs, out):
         load_x(2, 0)
         load_x(2, 1)
         load_w(0, 2)
-        load_w(2, 4)
         load_x(3, 0)
-        load_x(3, 1)
+        load_w(2, 4)
+        load_x(3, 1, 0)
+        load_x(3, 1, 1)
         load_w(4, 6)
         load_w(6, 8)
         load_w(8, 10)
@@ -84,13 +85,16 @@ def tile_moe_shr_lin_silu_kernel(tc, xT, w, b, gate, offs, out):
         xs_scales = [keep.tile([P, T], U8, name="xs_scales_%d" % c, align_bytes=64) for c in range(PASSES)]
         xr_codes = [keep.tile([P, S], U32, name="xr_codes_%d" % c, align_bytes=64) for c in range(PASSES)]
         xr_scales = [keep.tile([P, S], U8, name="xr_scales_%d" % c, align_bytes=64) for c in range(PASSES)]
-        w_bf = keep.tile([P, 12 * 512], BF16, name="w_bf", align_bytes=64)
-        w_codes = keep.tile([P, 12 * N], U32, name="w_codes", align_bytes=64)
+        w_bf = keep.tile([P, 8 * 512], BF16, name="w_bf", align_bytes=64)
+        late_codes = keep.tile([P, 8 * N], U32, name="late_codes", align_bytes=64)
         w_scales = keep.tile([P, 12 * N], U8, name="w_scales", align_bytes=64)
-        pp = [ring.tile([P, 4096], BF16, name="pp", align_bytes=64) for c in range(PASSES)]
-        g = [ring.tile([P, 2048], BF16, name="g", align_bytes=64) for c in range(PASSES)]
-        xs = [ring.tile([P, 4096], BF16, name="xs", align_bytes=64) for c in range(PASSES)]
-        xr = [ring.tile([P, 2048], BF16, name="xr", align_bytes=64) for c in range(PASSES)]
+        pp = [keep.tile([P, 4096], BF16, name="pp_%d" % c, tag="pairs_%d" % (c % 3), align_bytes=64) for c in range(PASSES)]
+        early_codes = [keep.tile([P, 2 * N], U32, name="early_codes_%d" % i, tag="gathered_%d" % i, align_bytes=64) for i in range(2)]
+        g = [keep.tile([P, 2048], BF16, name="g_%d" % c, tag="gathered_%d" % (c % 2), align_bytes=64) for c in range(PASSES)]
+        woven = [keep.tile([P, 6144], BF16, name="woven_%d" % c, align_bytes=64) for c in range(PASSES - 1)]
+        xs = [[woven[c][:, :2048], woven[c][:, 2048:4096]] for c in range(PASSES - 1)]
+        xs.append([w_raw[:, 6 * 512:8 * 512].bitcast(BF16), w_bf[:, :2048]])
+        xr = [woven[c % 3][:, 4096:] if c < 3 else woven[0][:, 4096:] for c in range(PASSES)]
 
 
         def planes(c, u, lo=0, hi=T, copy=nc.scalar.copy):
@@ -100,15 +104,34 @@ def tile_moe_shr_lin_silu_kernel(tc, xT, w, b, gate, offs, out):
             dst = pp[c][:, u * 2048 + 2 * lo:u * 2048 + 2 * hi].rearrange("p (t j) -> p t j", j=2)
             copy(dst, piece[:, lo - base:hi - base])
 
+        def w_codes(s):
+            if s.start < 4 * N:
+                i = s.start // (2 * N)
+                return early_codes[i][:, s.start - 2 * N * i:s.stop - 2 * N * i].bitcast(FP8X4)
+            return late_codes[:, s.start - 4 * N:s.stop - 4 * N].bitcast(FP8X4)
+
+        def staged(q0, q1):
+            if q0 < 4:
+                lo = 3584 + (q0 % 2) * 512
+                return woven[1 + q0 // 2][:, lo:lo + (q1 - q0) * 512]
+            return w_bf[:, (q0 - 4) * 512:(q1 - 4) * 512]
+
         def group_w(q0, q1, copy=nc.scalar.copy):
             copy(
-                w_bf[:, q0 * 512:q1 * 512].rearrange("p (q c i j) -> p q c j i", q=q1 - q0, i=4, j=4),
+                staged(q0, q1).rearrange("p (q c i j) -> p q c j i", q=q1 - q0, i=4, j=4),
                 w_raw[:, q0 * 512:q1 * 512].rearrange("p (q j c i) -> p q c j i", q=q1 - q0, i=4, j=4),
+            )
+
+        def group_w_gpsimd(q0, q1):
+            nc.gpsimd.tensor_scalar(
+                staged(q0, q1).rearrange("p (q n j) -> p q n j", q=q1 - q0, j=4),
+                w_raw[:, q0 * 512:q1 * 512].rearrange("p (q j n) -> p q n j", q=q1 - q0, j=4),
+                1.0, 0.0, MULT, ADD,
             )
 
         def quant_w(q0, q1):
             s = slice(q0 * N, q1 * N)
-            nc.vector.quantize_mx(out=w_codes[:, s].bitcast(FP8X4), scales=w_scales[:, s], in_=w_bf[:, q0 * 512:q1 * 512])
+            nc.vector.quantize_mx(out=w_codes(s), scales=w_scales[:, s], in_=staged(q0, q1))
 
         def gather(c, u):
             nc.vector.tensor_copy(
@@ -118,29 +141,29 @@ def tile_moe_shr_lin_silu_kernel(tc, xT, w, b, gate, offs, out):
 
         def inter_s(c, lo=0, hi=T, copy=nc.vector.tensor_copy, dt=F32):
             copy(
-                xs[c][:].bitcast(dt).rearrange("p (t u) -> p t u", u=2)[:, lo:hi],
+                xs[c][lo // 512].bitcast(dt).rearrange("p (t u) -> p t u", u=2),
                 pp[c][:].bitcast(dt).rearrange("p (u t) -> p t u", u=2)[:, lo:hi],
             )
 
         def inter_g(c, copy=nc.vector.tensor_copy):
             copy(
-                xr[c][:].bitcast(F32).rearrange("p (t u) -> p t u", u=2),
+                xr[c].bitcast(F32).rearrange("p (t u) -> p t u", u=2),
                 g[c][:].bitcast(F32).rearrange("p (u t) -> p t u", u=2),
             )
 
         def quant_r(c):
-            nc.vector.quantize_mx(out=xr_codes[c][:].bitcast(FP8X4), scales=xr_scales[c][:], in_=xr[c][:])
+            nc.vector.quantize_mx(out=xr_codes[c][:].bitcast(FP8X4), scales=xr_scales[c][:], in_=xr[c])
 
         def quant_s(c, lo=0, hi=T):
             nc.vector.quantize_mx(
-                out=xs_codes[c][:, lo:hi].bitcast(FP8X4), scales=xs_scales[c][:, lo:hi], in_=xs[c][:, 4 * lo:4 * hi])
+                out=xs_codes[c][:, lo:hi].bitcast(FP8X4), scales=xs_scales[c][:, lo:hi], in_=woven[c][:, :4096] if hi - lo == T else xs[c][lo // 512])
 
         def routed(c):
             for e in range(E):
                 q = slice(blocks.index((c, e)) * N, (blocks.index((c, e)) + 1) * N)
                 s = slice(e * C, (e + 1) * C)
                 nc.tensor.matmul_mx(
-                    out=acc_r[e][:], lhsT=w_codes[:, q].bitcast(FP8X4), lhsT_scale=w_scales[:, q],
+                    out=acc_r[e][:], lhsT=w_codes(q), lhsT_scale=w_scales[:, q],
                     rhs=xr_codes[c][:, s].bitcast(FP8X4), rhs_scale=xr_scales[c][:, s],
                     start=(c == 0), stop=(c == PASSES - 1),
                 )
@@ -149,7 +172,7 @@ def tile_moe_shr_lin_silu_kernel(tc, xT, w, b, gate, offs, out):
             q = slice(blocks.index((c, E)) * N, (blocks.index((c, E)) + 1) * N)
             s = slice(h * 512, (h + 1) * 512)
             nc.tensor.matmul_mx(
-                out=acc_s[h][:], lhsT=w_codes[:, q].bitcast(FP8X4), lhsT_scale=w_scales[:, q],
+                out=acc_s[h][:], lhsT=w_codes(q), lhsT_scale=w_scales[:, q],
                 rhs=xs_codes[c][:, s].bitcast(FP8X4), rhs_scale=xs_scales[c][:, s],
                 start=(c == 0), stop=(c == PASSES - 1),
             )
@@ -197,38 +220,42 @@ def tile_moe_shr_lin_silu_kernel(tc, xT, w, b, gate, offs, out):
         planes(2, 1)
         quant_s(1)
         quant_r(1)
+        group_w_gpsimd(0, 2)
         gather(2, 0)
         gather(2, 1)
-        inter_s(2)
+        inter_s(2, 0, 512, cs)
+        inter_s(2, 512, T)
         inter_g(2)
-        group_w(0, 4)
         planes(3, 0)
-        planes(3, 1)
+        planes(3, 1, 0, 512)
+        planes(3, 1, 512, T)
+        quant_w(0, 2)
+        routed(0)
         quant_s(2)
         quant_r(2)
+        group_w_gpsimd(2, 4)
         gather(3, 0)
-        quant_w(0, 4)
-        routed(0)
-        routed(1)
         gather(3, 1)
         group_w(4, 6)
         group_w(6, 8)
+        inter_s(3, 0, 512, cs)
         group_w(8, 10)
         group_w(10, 12)
-        inter_s(3, 0, 512)
         inter_g(3)
-        inter_s(3, 512, T)
+        quant_w(2, 4)
+        routed(1)
         quant_r(3)
         quant_w(4, 8)
         routed(2)
         routed(3)
         act_r(0)
         act_r(1)
+        inter_s(3, 512, T)
+        quant_s(3, 0, 512)
         quant_w(8, 10)
         for h in range(2):
             for c in range(2):
                 shared(c, h)
-        quant_s(3, 0, 512)
         quant_s(3, 512, T)
         quant_w(10, 12)
         for h in range(2):

@@ -85,15 +85,15 @@ def tile_moe_shr_lin_silu_kernel(tc, xT, w, b, gate, offs, out):
         xs_scales = [keep.tile([P, T], U8, name="xs_scales_%d" % c, align_bytes=64) for c in range(PASSES)]
         xr_codes = [keep.tile([P, S], U32, name="xr_codes_%d" % c, align_bytes=64) for c in range(PASSES)]
         xr_scales = [keep.tile([P, S], U8, name="xr_scales_%d" % c, align_bytes=64) for c in range(PASSES)]
-        w_bf = keep.tile([P, 8 * 512], BF16, name="w_bf", align_bytes=64)
-        late_codes = keep.tile([P, 8 * N], U32, name="late_codes", align_bytes=64)
+        w_bf = keep.tile([P, 6 * 512], BF16, name="w_bf", align_bytes=64)
+        late_codes = keep.tile([P, 10 * N], U32, name="late_codes", align_bytes=64)
         w_scales = keep.tile([P, 12 * N], U8, name="w_scales", align_bytes=64)
         pp = [keep.tile([P, 4096], BF16, name="pp_%d" % c, tag="pairs_%d" % (c % 3), align_bytes=64) for c in range(PASSES)]
-        early_codes = [keep.tile([P, 2 * N], U32, name="early_codes_%d" % i, tag="gathered_%d" % i, align_bytes=64) for i in range(2)]
+        early_codes = keep.tile([P, 2 * N], U32, name="early_codes", tag="gathered_0", align_bytes=64)
         g = [keep.tile([P, 2048], BF16, name="g_%d" % c, tag="gathered_%d" % (c % 2), align_bytes=64) for c in range(PASSES)]
         woven = [keep.tile([P, 6144], BF16, name="woven_%d" % c, align_bytes=64) for c in range(PASSES - 1)]
         xs = [[woven[c][:, :2048], woven[c][:, 2048:4096]] for c in range(PASSES - 1)]
-        xs.append([w_raw[:, 6 * 512:8 * 512].bitcast(BF16), w_bf[:, :2048]])
+        xs.append([w_raw[:, 6 * 512:8 * 512].bitcast(BF16), woven[1][:, :2048]])
         xr = [woven[c % 3][:, 4096:] if c < 3 else woven[0][:, 4096:] for c in range(PASSES)]
 
 
@@ -105,16 +105,16 @@ def tile_moe_shr_lin_silu_kernel(tc, xT, w, b, gate, offs, out):
             copy(dst, piece[:, lo - base:hi - base])
 
         def w_codes(s):
-            if s.start < 4 * N:
-                i = s.start // (2 * N)
-                return early_codes[i][:, s.start - 2 * N * i:s.stop - 2 * N * i].bitcast(FP8X4)
-            return late_codes[:, s.start - 4 * N:s.stop - 4 * N].bitcast(FP8X4)
+            if s.start < 2 * N:
+                return early_codes[:, s].bitcast(FP8X4)
+            return late_codes[:, s.start - 2 * N:s.stop - 2 * N].bitcast(FP8X4)
 
         def staged(q0, q1):
-            if q0 < 4:
-                lo = 3584 + (q0 % 2) * 512
-                return woven[1 + q0 // 2][:, lo:lo + (q1 - q0) * 512]
-            return w_bf[:, (q0 - 4) * 512:(q1 - 4) * 512]
+            if q0 < 2:
+                return woven[1][:, 3584 + q0 * 512:3584 + q1 * 512]
+            if q0 < 6:
+                return woven[2][:, 3584 + (q0 - 2) * 512:3584 + (q1 - 2) * 512]
+            return w_bf[:, (q0 - 6) * 512:(q1 - 6) * 512]
 
         def group_w(q0, q1, copy=nc.scalar.copy):
             copy(
@@ -241,22 +241,22 @@ def tile_moe_shr_lin_silu_kernel(tc, xT, w, b, gate, offs, out):
         inter_s(3, 0, 512, cs)
         group_w(8, 10)
         group_w(10, 12)
+        inter_s(3, 512, T)
         inter_g(3)
-        quant_w(2, 4)
+        quant_w(2, 6)
         routed(1)
-        quant_r(3)
-        quant_w(4, 8)
         routed(2)
+        quant_r(3)
+        quant_w(6, 8)
         routed(3)
         act_r(0)
         act_r(1)
-        inter_s(3, 512, T)
-        quant_s(3, 0, 512)
+        quant_s(3, 512, T)
         quant_w(8, 10)
         for h in range(2):
             for c in range(2):
                 shared(c, h)
-        quant_s(3, 512, T)
+        quant_s(3, 0, 512)
         quant_w(10, 12)
         for h in range(2):
             for c in range(2, 4):

@@ -141,14 +141,14 @@ def tile_moe_shr_lin_silu_kernel(tc, xT, w, b, gate, offs, out):
 
         def inter_s(c, lo=0, hi=T, copy=nc.vector.tensor_copy, dt=F32):
             copy(
-                xs[c][lo // 512].bitcast(dt).rearrange("p (t u) -> p t u", u=2),
-                pp[c][:].bitcast(dt).rearrange("p (u t) -> p t u", u=2)[:, lo:hi],
+                xs[c][lo // 512].bitcast(dt).rearrange("p (t i u) -> p t u i", i=2, u=2),
+                pp[c][:].bitcast(dt).rearrange("p (u t i) -> p t u i", i=2, u=2)[:, lo // 2:hi // 2],
             )
 
         def inter_g(c, copy=nc.vector.tensor_copy):
             copy(
-                xr[c].bitcast(F32).rearrange("p (t u) -> p t u", u=2),
-                g[c][:].bitcast(F32).rearrange("p (u t) -> p t u", u=2),
+                xr[c].bitcast(F32).rearrange("p (t i u) -> p t u i", i=2, u=2),
+                g[c][:].bitcast(F32).rearrange("p (u t i) -> p t u i", i=2, u=2),
             )
 
         def quant_r(c):

@@ -98,11 +98,12 @@ def tile_moe_shr_lin_silu_kernel(tc, xT, w, b, gate, offs, out):
 
 
         def planes(c, u, lo=0, hi=T, copy=nc.scalar.copy):
+            run = 1 if c == 0 else 4
             step = 512 if halved[(c, u)] else T
             base = lo // step * step
-            piece = x_raw[c][u][:, 2 * base:2 * (base + step)].rearrange("p (j t) -> p t j", j=2)
-            dst = pp[c][:, u * 2048 + 2 * lo:u * 2048 + 2 * hi].rearrange("p (t j) -> p t j", j=2)
-            copy(dst, piece[:, lo - base:hi - base])
+            piece = x_raw[c][u][:, 2 * base:2 * (base + step)].rearrange("p (j t i) -> p t j i", j=2, i=run)
+            dst = pp[c][:, u * 2048 + 2 * lo:u * 2048 + 2 * hi].rearrange("p (t i j) -> p t j i", j=2, i=run)
+            copy(dst, piece[:, (lo - base) // run:(hi - base) // run])
 
         def w_codes(s):
             if s.start < 2 * N:
@@ -139,10 +140,10 @@ def tile_moe_shr_lin_silu_kernel(tc, xT, w, b, gate, offs, out):
                 pp[c][:, u * 2048:(u + 1) * 2048].bitcast(U32).indirect(offsets[:]),
             )
 
-        def inter_s(c, lo=0, hi=T, copy=nc.vector.tensor_copy, dt=F32):
+        def inter_s(c, lo=0, hi=T, copy=nc.vector.tensor_copy, dt=F32, run=2):
             copy(
-                xs[c][lo // 512].bitcast(dt).rearrange("p (t i u) -> p t u i", i=2, u=2),
-                pp[c][:].bitcast(dt).rearrange("p (u t i) -> p t u i", i=2, u=2)[:, lo // 2:hi // 2],
+                xs[c][lo // 512].bitcast(dt).rearrange("p (t i u) -> p t u i", i=run, u=2),
+                pp[c][:].bitcast(dt).rearrange("p (u t i) -> p t u i", i=run, u=2)[:, lo // run:hi // run],
             )
 
         def inter_g(c, copy=nc.vector.tensor_copy):
@@ -198,7 +199,7 @@ def tile_moe_shr_lin_silu_kernel(tc, xT, w, b, gate, offs, out):
         cs, cv = nc.scalar.copy, nc.vector.tensor_copy
         planes(0, 0, 0, 512)
         planes(0, 1, 0, 512, cv)
-        inter_s(0, 0, 512)
+        inter_s(0, 0, 512, run=1)
         planes(0, 0, 512, T)
         quant_s(0, 0, 512)
         gather(0, 0)

@@ -6,6 +6,7 @@ K, T, E, C, N = 2048, 1024, 2, 256, 128
 S = E * C
 P = 128
 PASSES = K // 512
+H = T // 2
 FLOPS = 2 * K * N * (T + S)
 
 F32 = mybir.dt.float32
@@ -23,12 +24,12 @@ def tile_moe_shr_lin_silu_kernel(tc, xT, w, b, gate, offs, out):
     nc = tc.nc
     with ExitStack() as ctx:
         keep = ctx.enter_context(tc.tile_pool(name="keep", bufs=1))
-        ring = ctx.enter_context(tc.tile_pool(name="ring", bufs=3))
+        placed = ctx.enter_context(tc.tile_pool(name="placed", bufs=1))
         psum = ctx.enter_context(tc.psum_pool(name="psum", bufs=1))
 
         offsets = keep.tile([P, S // 16], U16, name="offsets")
         bias = keep.tile([P, E + 1], F32, name="bias")
-        gates = keep.tile([P, S], F32, name="gates")
+        gates = [keep.tile([P, C], F32, name="gates_%d" % e) for e in range(E)]
         scattered = keep.tile([P, T], F32, name="scattered")
         warm = keep.tile([P, 1], F32, name="warm")
 
@@ -36,234 +37,200 @@ def tile_moe_shr_lin_silu_kernel(tc, xT, w, b, gate, offs, out):
         nc.scalar.activation(warm[:], warm[:], SILU)
         nc.gpsimd.memset(scattered[:], 0.0)
 
-        x_raw = [[keep.tile([P, 2 * T], F32, name="x_raw_%d_%d" % (c, u)) for u in range(2)] for c in range(PASSES)]
-        blocks = [(c, e) for c in range(4) for e in range(2)] + [(c, 2) for c in range(4)]
-        w_raw = keep.tile([P, 12 * 512], F32, name="w_raw", align_bytes=64)
-        halved = {}
+        x_raw = [[[keep.tile([P, 2 * H], F32, name="x_raw_%d_%d_%d" % (c, h, u), tag="x_raw_%d_%d_%d" % (c, h, u), align_bytes=64) for u in range(2)]
+                  for h in range(2)] for c in range(PASSES)]
+        w_raw = [keep.tile([P, 2 * 512], F32, name="w_raw_%d" % i, tag="w_raw_%d" % i, align_bytes=64) if i != 3
+                 else placed.tile([P, 2 * 512], F32, name="w_raw_3", offset=0, align_bytes=64) for i in range(6)]
 
-        def load_x(c, u, half=None):
+        def load_x(c, h, u):
             rows = xT[c * 512:(c + 1) * 512, :].rearrange("(p j) t -> p j t", j=4)
-            lo, step = (0, T) if half is None else (half * 512, 512)
-            halved[(c, u)] = half is not None
-            dst = x_raw[c][u][:, 2 * lo:2 * (lo + step)].rearrange("p (j t) -> p j t", j=2)
-            nc.sync.dma_start(out=dst, in_=rows[:, 2 * u:2 * u + 2, lo:lo + step])
+            nc.sync.dma_start(out=x_raw[c][h][u][:].rearrange("p (j t) -> p j t", j=2),
+                              in_=rows[:, 2 * u:2 * u + 2, h * H:(h + 1) * H])
 
-        def load_w(q0, q1):
-            (c0, e0), (c1, e1) = blocks[q0], blocks[q1 - 1]
-            dst = w_raw[:, q0 * 512:q1 * 512].rearrange("p (q r) -> p q r", q=q1 - q0)
-            if c0 == c1:
-                src = w[e0:e1 + 1, c0 * 512:(c0 + 1) * 512, :].rearrange("e (p j) n -> p e (j n)", j=4)
-            else:
-                src = w[e0, c0 * 512:(c1 + 1) * 512, :].rearrange("(c p j) n -> p c (j n)", p=P, j=4)
-            nc.sync.dma_start(out=dst, in_=src)
+        def load_w(i):
+            e, c0 = divmod(2 * i, PASSES)
+            nc.sync.dma_start(
+                out=w_raw[i][:].rearrange("p (q r) -> p q r", q=2),
+                in_=w[e, c0 * 512:(c0 + 2) * 512, :].rearrange("(c p j) n -> p c (j n)", p=P, j=4))
 
         load_x(0, 0, 0)
-        load_x(0, 1, 0)
+        load_x(0, 0, 1)
         nc.sync.dma_start(offsets[:], offs)
         nc.scalar.dma_start(out=bias[:], in_=b)
-        load_x(0, 0, 1)
+        load_x(0, 1, 0)
         load_x(0, 1, 1)
-        for u in range(2):
+        for c in range(1, PASSES):
             for h in range(2):
-                load_x(1, u, h)
-        load_x(2, 0)
-        load_x(2, 1)
-        load_w(0, 2)
-        load_x(3, 0)
-        load_w(2, 4)
-        load_x(3, 1, 0)
-        load_x(3, 1, 1)
-        load_w(4, 6)
-        load_w(6, 8)
-        load_w(8, 10)
-        load_w(10, 12)
-        nc.sync.dma_start(gates[:], gate)
+                for u in range(2):
+                    load_x(c, h, u)
+        for i in (0, 1, 2, 4, 3):
+            load_w(i)
+        nc.sync.dma_start(gates[0][:], gate[:, :C])
+        load_w(5)
+        nc.sync.dma_start(gates[1][:], gate[:, C:])
 
         acc_r = [psum.tile([P, C], F32, name="acc_r_%d" % e) for e in range(E)]
         acc_s = [psum.tile([P, 512], F32, name="acc_s_%d" % h) for h in range(2)]
-        xs_codes = [keep.tile([P, T], U32, name="xs_codes_%d" % c, align_bytes=64) for c in range(PASSES)]
+        xs_codes = [[keep.tile([P, H], U32, name="xs_codes_%d_%d" % (c, h), align_bytes=64,
+                               tag="x_raw_%d_1_1" % c if (h == 0 and c > 0) else "xs_codes_%d_%d" % (c, h))
+                     for h in range(2)] for c in range(PASSES)]
         xs_scales = [keep.tile([P, T], U8, name="xs_scales_%d" % c, align_bytes=64) for c in range(PASSES)]
-        xr_codes = [keep.tile([P, S], U32, name="xr_codes_%d" % c, align_bytes=64) for c in range(PASSES)]
+        xr_codes = [keep.tile([P, S], U32, name="xr_codes_%d" % c, align_bytes=64,
+                              tag="w_raw_1" if c == PASSES - 1 else "xr_codes_%d" % c) for c in range(PASSES)]
         xr_scales = [keep.tile([P, S], U8, name="xr_scales_%d" % c, align_bytes=64) for c in range(PASSES)]
-        w_bf = keep.tile([P, 6 * 512], BF16, name="w_bf", align_bytes=64)
-        late_codes = keep.tile([P, 10 * N], U32, name="late_codes", align_bytes=64)
+        w_codes01 = keep.tile([P, 4 * N], U32, name="w_codes01", tag="w_codes01", align_bytes=64)
+        w_codes = [w_codes01[:, :2 * N], w_codes01[:, 2 * N:]]
+        for i in range(2, 6):
+            if i == 4:
+                w_codes.append(placed.tile([P, 2 * N], U32, name="w_codes_4", offset=2048, align_bytes=64)[:])
+            else:
+                w_codes.append(keep.tile([P, 2 * N], U32, name="w_codes_%d" % i, align_bytes=64)[:])
         w_scales = keep.tile([P, 12 * N], U8, name="w_scales", align_bytes=64)
-        pp = [keep.tile([P, 4096], BF16, name="pp_%d" % c, tag="pairs_%d" % (c % 3), align_bytes=64) for c in range(PASSES)]
-        early_codes = keep.tile([P, 2 * N], U32, name="early_codes", tag="gathered_0", align_bytes=64)
-        g = [keep.tile([P, 2048], BF16, name="g_%d" % c, tag="gathered_%d" % (c % 2), align_bytes=64) for c in range(PASSES)]
-        woven = [keep.tile([P, 6144], BF16, name="woven_%d" % c, align_bytes=64) for c in range(PASSES - 1)]
-        xs = [[woven[c][:, :2048], woven[c][:, 2048:4096]] for c in range(PASSES - 1)]
-        xs.append([w_raw[:, 6 * 512:8 * 512].bitcast(BF16), woven[1][:, :2048]])
-        xr = [woven[c % 3][:, 4096:] if c < 3 else woven[0][:, 4096:] for c in range(PASSES)]
+        w_bf01 = keep.tile([P, 4 * 512], BF16, name="w_bf01", align_bytes=64)
+        w_bf = [w_bf01[:, :1024], w_bf01[:, 1024:]]
+        for i in range(2, 6):
+            w_bf.append(keep.tile([P, 2 * 512], BF16, name="w_bf_%d" % i, align_bytes=64,
+                                  tag="w_codes01" if i == 5 else "w_bf_%d" % i)[:])
+        pairs = [keep.tile([P, 4 * T], BF16, name="pairs_%d" % c, align_bytes=64) for c in range(PASSES)]
+        gathered = keep.tile([P, 4 * S], BF16, name="gathered", align_bytes=64)
+        woven_s = [keep.tile([P, 4 * H], BF16, name="woven_s_%d" % i, align_bytes=64) for i in range(2)]
+        woven_r = keep.tile([P, 4 * S], BF16, name="woven_r", align_bytes=64)
 
-
-        def planes(c, u, lo=0, hi=T, copy=nc.scalar.copy):
+        def round_x(c, h, u, copy=nc.scalar.copy):
             run = 1 if c == 0 else 4
-            step = 512 if halved[(c, u)] else T
-            base = lo // step * step
-            piece = x_raw[c][u][:, 2 * base:2 * (base + step)].rearrange("p (j t i) -> p t j i", j=2, i=run)
-            dst = pp[c][:, u * 2048 + 2 * lo:u * 2048 + 2 * hi].rearrange("p (t i j) -> p t j i", j=2, i=run)
-            copy(dst, piece[:, (lo - base) // run:(hi - base) // run])
+            src = x_raw[c][h][u][:].rearrange("p (j t i) -> p t j i", j=2, i=run)
+            lo = u * 2 * T + h * 2 * H
+            copy(pairs[c][:, lo:lo + 2 * H].rearrange("p (t i j) -> p t j i", j=2, i=run), src)
 
-        def w_codes(s):
-            if s.start < 2 * N:
-                return early_codes[:, s].bitcast(FP8X4)
-            return late_codes[:, s.start - 2 * N:s.stop - 2 * N].bitcast(FP8X4)
-
-        def staged(q0, q1):
-            if q0 < 2:
-                return woven[1][:, 3584 + q0 * 512:3584 + q1 * 512]
-            if q0 < 6:
-                return woven[2][:, 3584 + (q0 - 2) * 512:3584 + (q1 - 2) * 512]
-            return w_bf[:, (q0 - 6) * 512:(q1 - 6) * 512]
-
-        def group_w(q0, q1, copy=nc.scalar.copy):
+        def round_w(i, copy=nc.scalar.copy):
             copy(
-                staged(q0, q1).rearrange("p (q c i j) -> p q c j i", q=q1 - q0, i=4, j=4),
-                w_raw[:, q0 * 512:q1 * 512].rearrange("p (q j c i) -> p q c j i", q=q1 - q0, i=4, j=4),
+                w_bf[i].rearrange("p (q c i j) -> p q c j i", q=2, i=4, j=4),
+                w_raw[i][:].rearrange("p (q j c i) -> p q c j i", q=2, i=4, j=4),
             )
 
-        def group_w_gpsimd(q0, q1):
-            nc.gpsimd.tensor_scalar(
-                staged(q0, q1).rearrange("p (q n j) -> p q n j", q=q1 - q0, j=4),
-                w_raw[:, q0 * 512:q1 * 512].rearrange("p (q j n) -> p q n j", q=q1 - q0, j=4),
-                1.0, 0.0, MULT, ADD,
-            )
-
-        def quant_w(q0, q1):
-            s = slice(q0 * N, q1 * N)
-            nc.vector.quantize_mx(out=w_codes(s), scales=w_scales[:, s], in_=staged(q0, q1))
+        def quant_w(i, both=False):
+            n = (4 if both else 2) * N
+            nc.vector.quantize_mx(out=(w_codes01[:] if both else w_codes[i]).bitcast(FP8X4),
+                                  scales=w_scales[:, i * 2 * N:i * 2 * N + n], in_=w_bf01[:] if both else w_bf[i])
 
         def gather(c, u):
             nc.vector.tensor_copy(
-                g[c][:, u * 1024:(u + 1) * 1024].bitcast(U32),
-                pp[c][:, u * 2048:(u + 1) * 2048].bitcast(U32).indirect(offsets[:]),
+                gathered[:, u * 2 * S:(u + 1) * 2 * S].bitcast(U32),
+                pairs[c][:, u * 2 * T:(u + 1) * 2 * T].bitcast(U32).indirect(offsets[:]),
             )
 
-        def inter_s(c, lo=0, hi=T, copy=nc.vector.tensor_copy, dt=F32, run=2):
+        def weave_s(c, lo, hi, copy, dt=F32):
+            half = woven_s[(c + lo // H) % 2]
+            base = lo // H * H
             copy(
-                xs[c][lo // 512].bitcast(dt).rearrange("p (t i u) -> p t u i", i=run, u=2),
-                pp[c][:].bitcast(dt).rearrange("p (u t i) -> p t u i", i=run, u=2)[:, lo // run:hi // run],
+                half[:, 4 * (lo - base):4 * (hi - base)].bitcast(dt).rearrange("p (t u) -> p t u", u=2),
+                pairs[c][:].bitcast(dt).rearrange("p (u t) -> p t u", u=2)[:, lo:hi],
             )
 
-        def inter_g(c, copy=nc.vector.tensor_copy):
-            copy(
-                xr[c].bitcast(F32).rearrange("p (t i u) -> p t u i", i=2, u=2),
-                g[c][:].bitcast(F32).rearrange("p (u t i) -> p t u i", i=2, u=2),
+        def weave_r(c):
+            nc.vector.tensor_copy(
+                woven_r[:].bitcast(F32).rearrange("p (t i u) -> p t u i", i=2, u=2),
+                gathered[:].bitcast(F32).rearrange("p (u t i) -> p t u i", i=2, u=2),
             )
 
         def quant_r(c):
-            nc.vector.quantize_mx(out=xr_codes[c][:].bitcast(FP8X4), scales=xr_scales[c][:], in_=xr[c])
+            nc.vector.quantize_mx(out=xr_codes[c][:].bitcast(FP8X4), scales=xr_scales[c][:], in_=woven_r[:])
 
-        def quant_s(c, lo=0, hi=T):
-            nc.vector.quantize_mx(
-                out=xs_codes[c][:, lo:hi].bitcast(FP8X4), scales=xs_scales[c][:, lo:hi], in_=woven[c][:, :4096] if hi - lo == T else xs[c][lo // 512])
+        def quant_s(c, h):
+            s = slice(h * H, (h + 1) * H)
+            nc.vector.quantize_mx(out=xs_codes[c][h][:].bitcast(FP8X4), scales=xs_scales[c][:, s],
+                                  in_=woven_s[(c + h) % 2][:])
 
-        def routed(c):
-            for e in range(E):
-                q = slice(blocks.index((c, e)) * N, (blocks.index((c, e)) + 1) * N)
-                s = slice(e * C, (e + 1) * C)
-                nc.tensor.matmul_mx(
-                    out=acc_r[e][:], lhsT=w_codes(q), lhsT_scale=w_scales[:, q],
-                    rhs=xr_codes[c][:, s].bitcast(FP8X4), rhs_scale=xr_scales[c][:, s],
-                    start=(c == 0), stop=(c == PASSES - 1),
-                )
-
-        def shared(c, h):
-            q = slice(blocks.index((c, E)) * N, (blocks.index((c, E)) + 1) * N)
-            s = slice(h * 512, (h + 1) * 512)
+        def routed(e, c):
+            q = slice((e * PASSES + c) * N, (e * PASSES + c + 1) * N)
+            s = slice(e * C, (e + 1) * C)
             nc.tensor.matmul_mx(
-                out=acc_s[h][:], lhsT=w_codes(q), lhsT_scale=w_scales[:, q],
-                rhs=xs_codes[c][:, s].bitcast(FP8X4), rhs_scale=xs_scales[c][:, s],
+                out=acc_r[e][:], lhsT=w_codes[2 * e + c // 2][:, c % 2 * N:(c % 2 + 1) * N].bitcast(FP8X4), lhsT_scale=w_scales[:, q],
+                rhs=xr_codes[c][:, s].bitcast(FP8X4), rhs_scale=xr_scales[c][:, s],
                 start=(c == 0), stop=(c == PASSES - 1),
             )
 
-        y = keep.tile([P, S], F32, name="y")
+        def shared(c, h):
+            q = slice((E * PASSES + c) * N, (E * PASSES + c + 1) * N)
+            s = slice(h * H, (h + 1) * H)
+            nc.tensor.matmul_mx(
+                out=acc_s[h][:], lhsT=w_codes[2 * E + c // 2][:, c % 2 * N:(c % 2 + 1) * N].bitcast(FP8X4), lhsT_scale=w_scales[:, q],
+                rhs=xs_codes[c][h][:].bitcast(FP8X4), rhs_scale=xs_scales[c][:, s],
+                start=(c == 0), stop=(c == PASSES - 1),
+            )
+
+        y = [placed.tile([P, C], F32, name="y_0", offset=0, align_bytes=64),
+             keep.tile([P, C], F32, name="y_1", tag="w_raw_5", align_bytes=64)]
         ys = keep.tile([P, T], F32, name="ys")
         res = keep.tile([P, T], F32, name="res")
 
         def act_r(e):
-            s = slice(e * C, (e + 1) * C)
-            nc.scalar.activation(y[:, s], acc_r[e][:], SILU, bias=bias[:, e:e + 1])
+            nc.scalar.activation(y[e][:], acc_r[e][:], SILU, bias=bias[:, e:e + 1])
 
-        def scatter_all():
-            nc.vector.tensor_tensor(scattered[:].indirect(offsets[:]), y[:], gates[:], MULT)
+        def scatter(e):
+            nc.vector.tensor_tensor(scattered[:].indirect(offsets[:, e * C // 16:(e + 1) * C // 16]), y[e][:], gates[e][:], MULT)
 
         def act_s(h):
-            nc.scalar.activation(ys[:, h * 512:(h + 1) * 512], acc_s[h][:], SILU, bias=bias[:, E:E + 1])
+            nc.scalar.activation(ys[:, h * H:(h + 1) * H], acc_s[h][:], SILU, bias=bias[:, E:E + 1])
 
-        def finish(lo, hi, queue=nc.sync):
-            nc.vector.tensor_tensor(res[:, lo:hi], ys[:, lo:hi], scattered[:, lo:hi], ADD)
-            queue.dma_start(out=out[:, lo:hi], in_=res[:, lo:hi])
+        def finish(h):
+            s = slice(h * H, (h + 1) * H)
+            nc.vector.tensor_tensor(res[:, s], ys[:, s], scattered[:, s], ADD)
+            nc.sync.dma_start(out=out[:, s], in_=res[:, s])
 
-        cs, cv = nc.scalar.copy, nc.vector.tensor_copy
-        planes(0, 0, 0, 512)
-        planes(0, 1, 0, 512, cv)
-        inter_s(0, 0, 512, run=1)
-        planes(0, 0, 512, T)
-        quant_s(0, 0, 512)
-        gather(0, 0)
-        planes(0, 1, 512, T)
-        gather(0, 1)
-        for u in range(2):
-            for h in range(2):
-                planes(1, u, h * 512, h * 512 + 512)
-        inter_s(0, 512, T)
-        inter_g(0)
-        quant_s(0, 512, T)
-        quant_r(0)
-        gather(1, 0)
-        gather(1, 1)
-        inter_s(1, 0, 512, cs)
-        inter_s(1, 512, T)
-        inter_g(1)
-        planes(2, 0)
-        planes(2, 1)
-        quant_s(1)
-        quant_r(1)
-        group_w_gpsimd(0, 2)
-        gather(2, 0)
-        gather(2, 1)
-        inter_s(2, 0, 512, cs)
-        inter_s(2, 512, T)
-        inter_g(2)
-        planes(3, 0)
-        planes(3, 1, 0, 512)
-        planes(3, 1, 512, T)
-        quant_w(0, 2)
-        routed(0)
-        quant_s(2)
-        quant_r(2)
-        group_w_gpsimd(2, 4)
-        gather(3, 0)
-        gather(3, 1)
-        group_w(4, 6)
-        group_w(6, 8)
-        inter_s(3, 0, 512, cs)
-        group_w(8, 10)
-        group_w(10, 12)
-        inter_s(3, 512, T)
-        inter_g(3)
-        quant_w(2, 6)
-        routed(1)
-        routed(2)
-        quant_r(3)
-        quant_w(6, 8)
-        routed(3)
+        cs, cv, cg = nc.scalar.copy, nc.vector.tensor_copy, nc.gpsimd.tensor_copy
+        for c in range(PASSES):
+            round_x(c, 0, 0)
+            round_x(c, 0, 1, cv if c == 0 else cs)
+            if c == 0:
+                weave_s(c, 0, H, cv)
+            round_x(c, 1, 0)
+            if c == 0:
+                quant_s(c, 0)
+            gather(c, 0)
+            if c > 0:
+                weave_s(c, 0, H, cg, U32)
+            round_x(c, 1, 1)
+            gather(c, 1)
+            if c > 0:
+                weave_s(c, H, H + 256, cg, U32)
+                quant_s(c, 0)
+            else:
+                weave_s(c, H, H + 256, cv)
+            weave_s(c, H + 256, T, cs)
+            weave_r(c)
+            quant_s(c, 1)
+            if c < PASSES - 1:
+                quant_r(c)
+        last = PASSES - 1
+        round_w(0)
+        round_w(1)
+        quant_w(0, True)
+        for c in range(last):
+            routed(0, c)
+        quant_r(last)
+        routed(0, last)
+        round_w(2)
+        round_w(3)
         act_r(0)
-        act_r(1)
-        quant_s(3, 512, T)
-        quant_w(8, 10)
+        round_w(4, cv)
+        quant_w(2)
+        quant_w(3)
+        for c in range(PASSES):
+            routed(1, c)
+        quant_w(4)
         for h in range(2):
             for c in range(2):
                 shared(c, h)
-        quant_s(3, 0, 512)
-        quant_w(10, 12)
+        scatter(0)
+        round_w(5)
+        act_r(1)
+        quant_w(5)
         for h in range(2):
             for c in range(2, 4):
                 shared(c, h)
-        scatter_all()
+        scatter(1)
         for h in range(2):
             act_s(h)
         for h in range(2):
-            finish(h * 512, h * 512 + 512)
+            finish(h)

@@ -24,12 +24,11 @@ def tile_moe_shr_lin_silu_kernel(tc, xT, w, b, gate, offs, out):
     nc = tc.nc
     with ExitStack() as ctx:
         keep = ctx.enter_context(tc.tile_pool(name="keep", bufs=1))
-        placed = ctx.enter_context(tc.tile_pool(name="placed", bufs=1))
         psum = ctx.enter_context(tc.psum_pool(name="psum", bufs=1))
 
         offsets = keep.tile([P, S // 16], U16, name="offsets")
         bias = keep.tile([P, E + 1], F32, name="bias")
-        gates = [keep.tile([P, C], F32, name="gates_%d" % e) for e in range(E)]
+        gates = keep.tile([P, S], F32, name="gates")
         scattered = keep.tile([P, T], F32, name="scattered")
         warm = keep.tile([P, 1], F32, name="warm")
 
@@ -37,10 +36,10 @@ def tile_moe_shr_lin_silu_kernel(tc, xT, w, b, gate, offs, out):
         nc.scalar.activation(warm[:], warm[:], SILU)
         nc.gpsimd.memset(scattered[:], 0.0)
 
-        x_raw = [[[keep.tile([P, 2 * H], F32, name="x_raw_%d_%d_%d" % (c, h, u), tag="x_raw_%d_%d_%d" % (c, h, u), align_bytes=64) for u in range(2)]
+        x_raw = [[[keep.tile([P, 2 * H], F32, name="x_raw_%d_%d_%d" % (c, h, u)) for u in range(2)]
                   for h in range(2)] for c in range(PASSES)]
-        w_raw = [keep.tile([P, 2 * 512], F32, name="w_raw_%d" % i, tag="w_raw_%d" % i, align_bytes=64) if i != 3
-                 else placed.tile([P, 2 * 512], F32, name="w_raw_3", offset=0, align_bytes=64) for i in range(6)]
+        order = [(0, 0), (1, 0), (0, 2), (1, 2), (2, 0), (2, 2)]
+        w_raw = [keep.tile([P, 2 * 512], F32, name="w_raw_%d" % i, tag="w_raw_%d" % i, align_bytes=64) for i in range(6)]
 
         def load_x(c, h, u):
             rows = xT[c * 512:(c + 1) * 512, :].rearrange("(p j) t -> p j t", j=4)
@@ -48,7 +47,7 @@ def tile_moe_shr_lin_silu_kernel(tc, xT, w, b, gate, offs, out):
                               in_=rows[:, 2 * u:2 * u + 2, h * H:(h + 1) * H])
 
         def load_w(i):
-            e, c0 = divmod(2 * i, PASSES)
+            e, c0 = order[i]
             nc.sync.dma_start(
                 out=w_raw[i][:].rearrange("p (q r) -> p q r", q=2),
                 in_=w[e, c0 * 512:(c0 + 2) * 512, :].rearrange("(c p j) n -> p c (j n)", p=P, j=4))
@@ -60,40 +59,29 @@ def tile_moe_shr_lin_silu_kernel(tc, xT, w, b, gate, offs, out):
         load_x(0, 1, 0)
         load_x(0, 1, 1)
         for c in range(1, PASSES):
+            if c == PASSES - 1:
+                load_w(0)
+                load_w(1)
             for h in range(2):
                 for u in range(2):
                     load_x(c, h, u)
-        for i in (0, 1, 2, 4, 3):
+        for i in range(2, 6):
             load_w(i)
-        nc.sync.dma_start(gates[0][:], gate[:, :C])
-        load_w(5)
-        nc.sync.dma_start(gates[1][:], gate[:, C:])
+        nc.sync.dma_start(gates[:], gate)
 
         acc_r = [psum.tile([P, C], F32, name="acc_r_%d" % e) for e in range(E)]
         acc_s = [psum.tile([P, 512], F32, name="acc_s_%d" % h) for h in range(2)]
-        xs_codes = [[keep.tile([P, H], U32, name="xs_codes_%d_%d" % (c, h), align_bytes=64,
-                               tag="x_raw_%d_1_1" % c if (h == 0 and c > 0) else "xs_codes_%d_%d" % (c, h))
-                     for h in range(2)] for c in range(PASSES)]
+        xs_codes = [keep.tile([P, T], U32, name="xs_codes_%d" % c, align_bytes=64,
+                              tag="w_raw_3" if c == PASSES - 1 else "xs_codes_%d" % c) for c in range(PASSES)]
         xs_scales = [keep.tile([P, T], U8, name="xs_scales_%d" % c, align_bytes=64) for c in range(PASSES)]
-        xr_codes = [keep.tile([P, S], U32, name="xr_codes_%d" % c, align_bytes=64,
-                              tag="w_raw_1" if c == PASSES - 1 else "xr_codes_%d" % c) for c in range(PASSES)]
+        xr_codes = [keep.tile([P, S], U32, name="xr_codes_%d" % c, align_bytes=64) for c in range(PASSES)]
         xr_scales = [keep.tile([P, S], U8, name="xr_scales_%d" % c, align_bytes=64) for c in range(PASSES)]
-        w_codes01 = keep.tile([P, 4 * N], U32, name="w_codes01", tag="w_codes01", align_bytes=64)
-        w_codes = [w_codes01[:, :2 * N], w_codes01[:, 2 * N:]]
-        for i in range(2, 6):
-            if i == 4:
-                w_codes.append(placed.tile([P, 2 * N], U32, name="w_codes_4", offset=2048, align_bytes=64)[:])
-            else:
-                w_codes.append(keep.tile([P, 2 * N], U32, name="w_codes_%d" % i, align_bytes=64)[:])
+        w_bf = keep.tile([P, 12 * 512], BF16, name="w_bf", align_bytes=64)
+        w_codes = keep.tile([P, 12 * N], U32, name="w_codes", align_bytes=64)
         w_scales = keep.tile([P, 12 * N], U8, name="w_scales", align_bytes=64)
-        w_bf01 = keep.tile([P, 4 * 512], BF16, name="w_bf01", align_bytes=64)
-        w_bf = [w_bf01[:, :1024], w_bf01[:, 1024:]]
-        for i in range(2, 6):
-            w_bf.append(keep.tile([P, 2 * 512], BF16, name="w_bf_%d" % i, align_bytes=64,
-                                  tag="w_codes01" if i == 5 else "w_bf_%d" % i)[:])
         pairs = [keep.tile([P, 4 * T], BF16, name="pairs_%d" % c, align_bytes=64) for c in range(PASSES)]
         gathered = keep.tile([P, 4 * S], BF16, name="gathered", align_bytes=64)
-        woven_s = [keep.tile([P, 4 * H], BF16, name="woven_s_%d" % i, align_bytes=64) for i in range(2)]
+        woven_s = keep.tile([P, 4 * T], BF16, name="woven_s", align_bytes=64)
         woven_r = keep.tile([P, 4 * S], BF16, name="woven_r", align_bytes=64)
 
         def round_x(c, h, u, copy=nc.scalar.copy):
@@ -102,16 +90,19 @@ def tile_moe_shr_lin_silu_kernel(tc, xT, w, b, gate, offs, out):
             lo = u * 2 * T + h * 2 * H
             copy(pairs[c][:, lo:lo + 2 * H].rearrange("p (t i j) -> p t j i", j=2, i=run), src)
 
-        def round_w(i, copy=nc.scalar.copy):
-            copy(
-                w_bf[i].rearrange("p (q c i j) -> p q c j i", q=2, i=4, j=4),
+        def round_w(i):
+            nc.scalar.copy(
+                w_bf[:, i * 1024:(i + 1) * 1024].rearrange("p (q c i j) -> p q c j i", q=2, i=4, j=4),
                 w_raw[i][:].rearrange("p (q j c i) -> p q c j i", q=2, i=4, j=4),
             )
 
-        def quant_w(i, both=False):
-            n = (4 if both else 2) * N
-            nc.vector.quantize_mx(out=(w_codes01[:] if both else w_codes[i]).bitcast(FP8X4),
-                                  scales=w_scales[:, i * 2 * N:i * 2 * N + n], in_=w_bf01[:] if both else w_bf[i])
+        def quant_w(g):
+            s = slice(g * 4 * N, (g + 1) * 4 * N)
+            nc.vector.quantize_mx(out=w_codes[:, s].bitcast(FP8X4), scales=w_scales[:, s], in_=w_bf[:, g * 2048:(g + 1) * 2048])
+
+        def block(e, c):
+            q = 2 * order.index((e, c // 2 * 2)) + c % 2
+            return slice(q * N, (q + 1) * N)
 
         def gather(c, u):
             nc.vector.tensor_copy(
@@ -119,15 +110,17 @@ def tile_moe_shr_lin_silu_kernel(tc, xT, w, b, gate, offs, out):
                 pairs[c][:, u * 2 * T:(u + 1) * 2 * T].bitcast(U32).indirect(offsets[:]),
             )
 
-        def weave_s(c, lo, hi, copy, dt=F32):
-            half = woven_s[(c + lo // H) % 2]
-            base = lo // H * H
+        def staged(c, h):
+            h = 1 - h if c == 0 else h
+            return woven_s[:, 4 * h * H:4 * (h + 1) * H]
+
+        def weave_s(c, h, copy, dt):
             copy(
-                half[:, 4 * (lo - base):4 * (hi - base)].bitcast(dt).rearrange("p (t u) -> p t u", u=2),
-                pairs[c][:].bitcast(dt).rearrange("p (u t) -> p t u", u=2)[:, lo:hi],
+                staged(c, h).bitcast(dt).rearrange("p (t u) -> p t u", u=2),
+                pairs[c][:].bitcast(dt).rearrange("p (u t) -> p t u", u=2)[:, h * H:(h + 1) * H],
             )
 
-        def weave_r(c):
+        def weave_r():
             nc.vector.tensor_copy(
                 woven_r[:].bitcast(F32).rearrange("p (t i u) -> p t u i", i=2, u=2),
                 gathered[:].bitcast(F32).rearrange("p (u t i) -> p t u i", i=2, u=2),
@@ -136,39 +129,39 @@ def tile_moe_shr_lin_silu_kernel(tc, xT, w, b, gate, offs, out):
         def quant_r(c):
             nc.vector.quantize_mx(out=xr_codes[c][:].bitcast(FP8X4), scales=xr_scales[c][:], in_=woven_r[:])
 
-        def quant_s(c, h):
-            s = slice(h * H, (h + 1) * H)
-            nc.vector.quantize_mx(out=xs_codes[c][h][:].bitcast(FP8X4), scales=xs_scales[c][:, s],
-                                  in_=woven_s[(c + h) % 2][:])
+        def quant_s(c, h=None):
+            s = slice(0, T) if h is None else slice(h * H, (h + 1) * H)
+            nc.vector.quantize_mx(out=xs_codes[c][:, s].bitcast(FP8X4), scales=xs_scales[c][:, s],
+                                  in_=woven_s[:] if h is None else staged(c, h))
 
         def routed(e, c):
-            q = slice((e * PASSES + c) * N, (e * PASSES + c + 1) * N)
+            q = block(e, c)
             s = slice(e * C, (e + 1) * C)
             nc.tensor.matmul_mx(
-                out=acc_r[e][:], lhsT=w_codes[2 * e + c // 2][:, c % 2 * N:(c % 2 + 1) * N].bitcast(FP8X4), lhsT_scale=w_scales[:, q],
+                out=acc_r[e][:], lhsT=w_codes[:, q].bitcast(FP8X4), lhsT_scale=w_scales[:, q],
                 rhs=xr_codes[c][:, s].bitcast(FP8X4), rhs_scale=xr_scales[c][:, s],
                 start=(c == 0), stop=(c == PASSES - 1),
             )
 
         def shared(c, h):
-            q = slice((E * PASSES + c) * N, (E * PASSES + c + 1) * N)
+            q = block(E, c)
             s = slice(h * H, (h + 1) * H)
             nc.tensor.matmul_mx(
-                out=acc_s[h][:], lhsT=w_codes[2 * E + c // 2][:, c % 2 * N:(c % 2 + 1) * N].bitcast(FP8X4), lhsT_scale=w_scales[:, q],
-                rhs=xs_codes[c][h][:].bitcast(FP8X4), rhs_scale=xs_scales[c][:, s],
+                out=acc_s[h][:], lhsT=w_codes[:, q].bitcast(FP8X4), lhsT_scale=w_scales[:, q],
+                rhs=xs_codes[c][:, s].bitcast(FP8X4), rhs_scale=xs_scales[c][:, s],
                 start=(c == 0), stop=(c == PASSES - 1),
             )
 
-        y = [placed.tile([P, C], F32, name="y_0", offset=0, align_bytes=64),
-             keep.tile([P, C], F32, name="y_1", tag="w_raw_5", align_bytes=64)]
+        y = keep.tile([P, S], F32, name="y", tag="w_raw_5", align_bytes=64)
         ys = keep.tile([P, T], F32, name="ys")
         res = keep.tile([P, T], F32, name="res")
 
         def act_r(e):
-            nc.scalar.activation(y[e][:], acc_r[e][:], SILU, bias=bias[:, e:e + 1])
+            s = slice(e * C, (e + 1) * C)
+            nc.scalar.activation(y[:, s], acc_r[e][:], SILU, bias=bias[:, e:e + 1])
 
-        def scatter(e):
-            nc.vector.tensor_tensor(scattered[:].indirect(offsets[:, e * C // 16:(e + 1) * C // 16]), y[e][:], gates[e][:], MULT)
+        def scatter():
+            nc.vector.tensor_tensor(scattered[:].indirect(offsets[:]), y[:], gates[:], MULT)
 
         def act_s(h):
             nc.scalar.activation(ys[:, h * H:(h + 1) * H], acc_s[h][:], SILU, bias=bias[:, E:E + 1])
@@ -179,57 +172,48 @@ def tile_moe_shr_lin_silu_kernel(tc, xT, w, b, gate, offs, out):
             nc.sync.dma_start(out=out[:, s], in_=res[:, s])
 
         cs, cv, cg = nc.scalar.copy, nc.vector.tensor_copy, nc.gpsimd.tensor_copy
+        last = PASSES - 1
         for c in range(PASSES):
+            if c == last:
+                round_w(0)
+                round_w(1)
+                quant_w(0)
+                for k in range(2):
+                    for e in range(E):
+                        routed(e, k)
             round_x(c, 0, 0)
             round_x(c, 0, 1, cv if c == 0 else cs)
             if c == 0:
-                weave_s(c, 0, H, cv)
+                weave_s(c, 0, cv, F32)
             round_x(c, 1, 0)
             if c == 0:
                 quant_s(c, 0)
             gather(c, 0)
             if c > 0:
-                weave_s(c, 0, H, cg, U32)
+                weave_s(c, 0, cg, U32)
             round_x(c, 1, 1)
             gather(c, 1)
-            if c > 0:
-                weave_s(c, H, H + 256, cg, U32)
-                quant_s(c, 0)
-            else:
-                weave_s(c, H, H + 256, cv)
-            weave_s(c, H + 256, T, cs)
-            weave_r(c)
-            quant_s(c, 1)
-            if c < PASSES - 1:
-                quant_r(c)
-        last = PASSES - 1
-        round_w(0)
-        round_w(1)
-        quant_w(0, True)
-        for c in range(last):
-            routed(0, c)
-        quant_r(last)
-        routed(0, last)
+            weave_s(c, 1, cg, U32)
+            weave_r()
+            if c < last:
+                quant_s(c, 1 if c == 0 else None)
+            quant_r(c)
         round_w(2)
         round_w(3)
-        act_r(0)
-        round_w(4, cv)
-        quant_w(2)
-        quant_w(3)
-        for c in range(PASSES):
-            routed(1, c)
-        quant_w(4)
-        for h in range(2):
-            for c in range(2):
-                shared(c, h)
-        scatter(0)
+        quant_w(1)
+        for e in range(E):
+            for c in range(2, PASSES):
+                routed(e, c)
+        quant_s(last)
+        round_w(4)
         round_w(5)
+        act_r(0)
         act_r(1)
-        quant_w(5)
+        quant_w(2)
         for h in range(2):
-            for c in range(2, 4):
+            for c in range(PASSES):
                 shared(c, h)
-        scatter(1)
+        scatter()
         for h in range(2):
             act_s(h)
         for h in range(2):

@@ -38,8 +38,9 @@ def tile_moe_shr_lin_silu_kernel(tc, xT, w, b, gate, offs, out):
 
         x_raw = [[[keep.tile([P, 2 * H], F32, name="x_raw_%d_%d_%d" % (c, h, u)) for u in range(2)]
                   for h in range(2)] for c in range(PASSES)]
-        order = [(0, 0), (1, 0), (0, 2), (1, 2), (2, 0), (2, 2)]
-        w_raw = [keep.tile([P, 2 * 512], F32, name="w_raw_%d" % i, tag="w_raw_%d" % i, align_bytes=64) for i in range(6)]
+        w_raw = [keep.tile([P, 2 * 512], F32, name="w_raw_%d" % i, tag="w_raw_%d" % i, align_bytes=64) for i in range(4)]
+        w_shared = keep.tile([P, 4 * 512], F32, name="w_shared", align_bytes=64)
+        w_raw = [t[:] for t in w_raw] + [w_shared[:, :1024], w_shared[:, 1024:]]
 
         def load_x(c, h, u):
             rows = xT[c * 512:(c + 1) * 512, :].rearrange("(p j) t -> p j t", j=4)
@@ -47,10 +48,12 @@ def tile_moe_shr_lin_silu_kernel(tc, xT, w, b, gate, offs, out):
                               in_=rows[:, 2 * u:2 * u + 2, h * H:(h + 1) * H])
 
         def load_w(i):
-            e, c0 = order[i]
-            nc.sync.dma_start(
-                out=w_raw[i][:].rearrange("p (q r) -> p q r", q=2),
-                in_=w[e, c0 * 512:(c0 + 2) * 512, :].rearrange("(c p j) n -> p c (j n)", p=P, j=4))
+            if i < PASSES:
+                src = w[:E, i * 512:(i + 1) * 512, :].rearrange("e (p j) n -> p e (j n)", j=4)
+            else:
+                c0 = 2 * (i - PASSES)
+                src = w[E, c0 * 512:(c0 + 2) * 512, :].rearrange("(c p j) n -> p c (j n)", p=P, j=4)
+            nc.sync.dma_start(out=w_raw[i].rearrange("p (q r) -> p q r", q=2), in_=src)
 
         load_x(0, 0, 0)
         load_x(0, 0, 1)
@@ -61,22 +64,24 @@ def tile_moe_shr_lin_silu_kernel(tc, xT, w, b, gate, offs, out):
         for c in range(1, PASSES):
             if c == PASSES - 1:
                 load_w(0)
-                load_w(1)
             for h in range(2):
                 for u in range(2):
                     load_x(c, h, u)
-        for i in range(2, 6):
+        for i in range(1, 5):
             load_w(i)
         nc.sync.dma_start(gates[:], gate)
+        load_w(5)
 
         acc_r = [psum.tile([P, C], F32, name="acc_r_%d" % e) for e in range(E)]
         acc_s = [psum.tile([P, 512], F32, name="acc_s_%d" % h) for h in range(2)]
         xs_codes = [keep.tile([P, T], U32, name="xs_codes_%d" % c, align_bytes=64,
                               tag="w_raw_3" if c == PASSES - 1 else "xs_codes_%d" % c) for c in range(PASSES)]
         xs_scales = [keep.tile([P, T], U8, name="xs_scales_%d" % c, align_bytes=64) for c in range(PASSES)]
-        xr_codes = [keep.tile([P, S], U32, name="xr_codes_%d" % c, align_bytes=64) for c in range(PASSES)]
+        xr_codes = [keep.tile([P, S], U32, name="xr_codes_%d" % c, align_bytes=64,
+                              tag="w_raw_2" if c == PASSES - 1 else "xr_codes_%d" % c) for c in range(PASSES)]
         xr_scales = [keep.tile([P, S], U8, name="xr_scales_%d" % c, align_bytes=64) for c in range(PASSES)]
-        w_bf = keep.tile([P, 12 * 512], BF16, name="w_bf", align_bytes=64)
+        w_bf = keep.tile([P, 10 * 512], BF16, name="w_bf", align_bytes=64)
+        w_bf_last = keep.tile([P, 2 * 512], BF16, name="w_bf_last", tag="w_raw_2", align_bytes=64)
         w_codes = keep.tile([P, 12 * N], U32, name="w_codes", align_bytes=64)
         w_scales = keep.tile([P, 12 * N], U8, name="w_scales", align_bytes=64)
         pairs = [keep.tile([P, 4 * T], BF16, name="pairs_%d" % c, align_bytes=64) for c in range(PASSES)]
@@ -90,18 +95,18 @@ def tile_moe_shr_lin_silu_kernel(tc, xT, w, b, gate, offs, out):
             lo = u * 2 * T + h * 2 * H
             copy(pairs[c][:, lo:lo + 2 * H].rearrange("p (t i j) -> p t j i", j=2, i=run), src)
 
-        def round_w(i):
-            nc.scalar.copy(
-                w_bf[:, i * 1024:(i + 1) * 1024].rearrange("p (q c i j) -> p q c j i", q=2, i=4, j=4),
-                w_raw[i][:].rearrange("p (q j c i) -> p q c j i", q=2, i=4, j=4),
+        def round_w(i, copy=nc.scalar.copy):
+            copy(
+                (w_bf_last[:] if i == 5 else w_bf[:, i * 1024:(i + 1) * 1024]).rearrange("p (q c i j) -> p q c j i", q=2, i=4, j=4),
+                w_raw[i].rearrange("p (q j c i) -> p q c j i", q=2, i=4, j=4),
             )
 
-        def quant_w(g):
-            s = slice(g * 4 * N, (g + 1) * 4 * N)
-            nc.vector.quantize_mx(out=w_codes[:, s].bitcast(FP8X4), scales=w_scales[:, s], in_=w_bf[:, g * 2048:(g + 1) * 2048])
+        def quant_w(i, n=1):
+            s = slice(i * 2 * N, (i + n) * 2 * N)
+            nc.vector.quantize_mx(out=w_codes[:, s].bitcast(FP8X4), scales=w_scales[:, s], in_=w_bf_last[:] if i == 5 else w_bf[:, i * 1024:(i + n) * 1024])
 
         def block(e, c):
-            q = 2 * order.index((e, c // 2 * 2)) + c % 2
+            q = 2 * c + e if e < E else 2 * PASSES + c
             return slice(q * N, (q + 1) * N)
 
         def gather(c, u):
@@ -152,7 +157,7 @@ def tile_moe_shr_lin_silu_kernel(tc, xT, w, b, gate, offs, out):
                 start=(c == 0), stop=(c == PASSES - 1),
             )
 
-        y = keep.tile([P, S], F32, name="y", tag="w_raw_5", align_bytes=64)
+        y = w_shared[:, 1024 - C:1024 + C]
         ys = keep.tile([P, T], F32, name="ys")
         res = keep.tile([P, T], F32, name="res")
 
@@ -160,8 +165,8 @@ def tile_moe_shr_lin_silu_kernel(tc, xT, w, b, gate, offs, out):
             s = slice(e * C, (e + 1) * C)
             nc.scalar.activation(y[:, s], acc_r[e][:], SILU, bias=bias[:, e:e + 1])
 
-        def scatter():
-            nc.vector.tensor_tensor(scattered[:].indirect(offsets[:]), y[:], gates[:], MULT)
+        def scatter(lo, hi):
+            nc.vector.tensor_tensor(scattered[:].indirect(offsets[:, lo // 16:hi // 16]), y[:, lo:hi], gates[:, lo:hi], MULT)
 
         def act_s(h):
             nc.scalar.activation(ys[:, h * H:(h + 1) * H], acc_s[h][:], SILU, bias=bias[:, E:E + 1])
@@ -176,11 +181,9 @@ def tile_moe_shr_lin_silu_kernel(tc, xT, w, b, gate, offs, out):
         for c in range(PASSES):
             if c == last:
                 round_w(0)
-                round_w(1)
                 quant_w(0)
-                for k in range(2):
-                    for e in range(E):
-                        routed(e, k)
+                for e in range(E):
+                    routed(e, 0)
             round_x(c, 0, 0)
             round_x(c, 0, 1, cv if c == 0 else cs)
             if c == 0:
@@ -197,23 +200,31 @@ def tile_moe_shr_lin_silu_kernel(tc, xT, w, b, gate, offs, out):
             weave_r()
             if c < last:
                 quant_s(c, 1 if c == 0 else None)
-            quant_r(c)
+                quant_r(c)
+        round_w(1)
         round_w(2)
+        quant_w(1, 2)
+        quant_r(last)
         round_w(3)
-        quant_w(1)
-        for e in range(E):
-            for c in range(2, PASSES):
+        quant_w(3)
+        for c in range(1, PASSES):
+            for e in range(E):
                 routed(e, c)
         quant_s(last)
         round_w(4)
-        round_w(5)
         act_r(0)
-        act_r(1)
-        quant_w(2)
+        quant_w(4)
         for h in range(2):
-            for c in range(PASSES):
+            for c in range(2):
                 shared(c, h)
-        scatter()
+        scatter(0, 192)
+        round_w(5)
+        act_r(1)
+        quant_w(5)
+        for h in range(2):
+            for c in range(2, PASSES):
+                shared(c, h)
+        scatter(192, S)
         for h in range(2):
             act_s(h)
         for h in range(2):

@@ -22,8 +22,10 @@ ADD = mybir.AluOpType.add
 
 def tile_moe_shr_lin_silu_kernel(tc, xT, w, b, gate, offs, out):
     nc = tc.nc
+    last = PASSES - 1
     with ExitStack() as ctx:
         keep = ctx.enter_context(tc.tile_pool(name="keep", bufs=1))
+        reuse = ctx.enter_context(tc.tile_pool(name="reuse", bufs=1))
         psum = ctx.enter_context(tc.psum_pool(name="psum", bufs=1))
 
         offsets = keep.tile([P, S // 16], U16, name="offsets")
@@ -32,15 +34,14 @@ def tile_moe_shr_lin_silu_kernel(tc, xT, w, b, gate, offs, out):
         scattered = keep.tile([P, T], F32, name="scattered")
         warm = keep.tile([P, 1], F32, name="warm")
 
+        nc.scalar.dma_start(out=bias[:], in_=b)
         nc.gpsimd.memset(warm[:], 0.0)
         nc.scalar.activation(warm[:], warm[:], SILU)
         nc.gpsimd.memset(scattered[:], 0.0)
 
-        x_raw = [[[keep.tile([P, 2 * H], F32, name="x_raw_%d_%d_%d" % (c, h, u)) for u in range(2)]
+        x_raw = [[[keep.tile([P, 2 * H], F32, name="x_raw_%d_%d_%d" % (c, h, u), tag="x_raw_%d_%d_%d" % (c, h, u), align_bytes=64) for u in range(2)]
                   for h in range(2)] for c in range(PASSES)]
-        w_raw = [keep.tile([P, 2 * 512], F32, name="w_raw_%d" % i, tag="w_raw_%d" % i, align_bytes=64) for i in range(4)]
-        w_shared = keep.tile([P, 4 * 512], F32, name="w_shared", align_bytes=64)
-        w_raw = [t[:] for t in w_raw] + [w_shared[:, :1024], w_shared[:, 1024:]]
+        w_raw = [reuse.tile([P, 1024], F32, name="w_raw_%d" % i, align_bytes=64, offset=4096 * i) for i in range(6)]
 
         def load_x(c, h, u):
             rows = xT[c * 512:(c + 1) * 512, :].rearrange("(p j) t -> p j t", j=4)
@@ -48,46 +49,45 @@ def tile_moe_shr_lin_silu_kernel(tc, xT, w, b, gate, offs, out):
                               in_=rows[:, 2 * u:2 * u + 2, h * H:(h + 1) * H])
 
         def load_w(i):
-            if i < PASSES:
-                src = w[:E, i * 512:(i + 1) * 512, :].rearrange("e (p j) n -> p e (j n)", j=4)
-            else:
-                c0 = 2 * (i - PASSES)
-                src = w[E, c0 * 512:(c0 + 2) * 512, :].rearrange("(c p j) n -> p c (j n)", p=P, j=4)
-            nc.sync.dma_start(out=w_raw[i].rearrange("p (q r) -> p q r", q=2), in_=src)
+            e, k0 = i // 2, (i % 2) * 1024
+            nc.sync.dma_start(out=w_raw[i][:].rearrange("p (q r) -> p q r", q=2),
+                              in_=w[e, k0:k0 + 1024, :].rearrange("(c p j) n -> p c (j n)", p=P, j=4))
 
         load_x(0, 0, 0)
         load_x(0, 0, 1)
         nc.sync.dma_start(offsets[:], offs)
-        nc.scalar.dma_start(out=bias[:], in_=b)
         load_x(0, 1, 0)
         load_x(0, 1, 1)
         for c in range(1, PASSES):
-            if c == PASSES - 1:
-                load_w(0)
             for h in range(2):
                 for u in range(2):
                     load_x(c, h, u)
-        for i in range(1, 5):
+        for i in range(5):
             load_w(i)
-        nc.sync.dma_start(gates[:], gate)
+        nc.sync.dma_start(out=gates[:], in_=gate)
         load_w(5)
 
         acc_r = [psum.tile([P, C], F32, name="acc_r_%d" % e) for e in range(E)]
         acc_s = [psum.tile([P, 512], F32, name="acc_s_%d" % h) for h in range(2)]
-        xs_codes = [keep.tile([P, T], U32, name="xs_codes_%d" % c, align_bytes=64,
-                              tag="w_raw_3" if c == PASSES - 1 else "xs_codes_%d" % c) for c in range(PASSES)]
-        xs_scales = [keep.tile([P, T], U8, name="xs_scales_%d" % c, align_bytes=64) for c in range(PASSES)]
+        xs_codes = [keep.tile([P, T], U32, name="xs_codes_%d" % c, align_bytes=64) for c in range(PASSES)]
+        xs_scales = [keep.tile([P, T], U8, name="xs_scales_%d" % c, align_bytes=64) for c in range(last)]
+        xs_scales_last = [reuse.tile([P, H], U8, name="xs_scales_last_%d" % h, align_bytes=64, offset=(4096 + 2048, 3 * 4096)[h])
+                          for h in range(2)]
+
+        def shared_scales(c, s):
+            return xs_scales[c][:, s] if c < last else xs_scales_last[s.start // H][:]
+
         xr_codes = [keep.tile([P, S], U32, name="xr_codes_%d" % c, align_bytes=64,
-                              tag="w_raw_2" if c == PASSES - 1 else "xr_codes_%d" % c) for c in range(PASSES)]
+                              tag="x_raw_%d_1_1" % (c + 1) if c > 0 else "xr_codes_0") for c in range(last)]
+        xr_codes.append(reuse.tile([P, S], U32, name="xr_codes_last", align_bytes=64, offset=4096))
         xr_scales = [keep.tile([P, S], U8, name="xr_scales_%d" % c, align_bytes=64) for c in range(PASSES)]
-        w_bf = keep.tile([P, 10 * 512], BF16, name="w_bf", align_bytes=64)
-        w_bf_last = keep.tile([P, 2 * 512], BF16, name="w_bf_last", tag="w_raw_2", align_bytes=64)
+        w_bf = keep.tile([P, 12 * 512], BF16, name="w_bf", align_bytes=64)
         w_codes = keep.tile([P, 12 * N], U32, name="w_codes", align_bytes=64)
         w_scales = keep.tile([P, 12 * N], U8, name="w_scales", align_bytes=64)
         pairs = [keep.tile([P, 4 * T], BF16, name="pairs_%d" % c, align_bytes=64) for c in range(PASSES)]
-        gathered = keep.tile([P, 4 * S], BF16, name="gathered", align_bytes=64)
         woven_s = keep.tile([P, 4 * T], BF16, name="woven_s", align_bytes=64)
-        woven_r = keep.tile([P, 4 * S], BF16, name="woven_r", align_bytes=64)
+        gathered = keep.tile([P, 4 * S], BF16, name="gathered", align_bytes=64)
+        woven_r = [keep.tile([P, 4 * S], BF16, name="woven_r_%d" % c, align_bytes=64) for c in range(2)]
 
         def round_x(c, h, u, copy=nc.scalar.copy):
             run = 1 if c == 0 else 4
@@ -95,19 +95,15 @@ def tile_moe_shr_lin_silu_kernel(tc, xT, w, b, gate, offs, out):
             lo = u * 2 * T + h * 2 * H
             copy(pairs[c][:, lo:lo + 2 * H].rearrange("p (t i j) -> p t j i", j=2, i=run), src)
 
-        def round_w(i, copy=nc.scalar.copy):
-            copy(
-                (w_bf_last[:] if i == 5 else w_bf[:, i * 1024:(i + 1) * 1024]).rearrange("p (q c i j) -> p q c j i", q=2, i=4, j=4),
-                w_raw[i].rearrange("p (q j c i) -> p q c j i", q=2, i=4, j=4),
+        def round_w(i):
+            nc.scalar.copy(
+                w_bf[:, i * 1024:(i + 1) * 1024].rearrange("p (q c i j) -> p q c j i", q=2, i=4, j=4),
+                w_raw[i][:].rearrange("p (q j c i) -> p q c j i", q=2, i=4, j=4),
             )
 
         def quant_w(i, n=1):
             s = slice(i * 2 * N, (i + n) * 2 * N)
-            nc.vector.quantize_mx(out=w_codes[:, s].bitcast(FP8X4), scales=w_scales[:, s], in_=w_bf_last[:] if i == 5 else w_bf[:, i * 1024:(i + n) * 1024])
-
-        def block(e, c):
-            q = 2 * c + e if e < E else 2 * PASSES + c
-            return slice(q * N, (q + 1) * N)
+            nc.vector.quantize_mx(out=w_codes[:, s].bitcast(FP8X4), scales=w_scales[:, s], in_=w_bf[:, i * 1024:(i + n) * 1024])
 
         def gather(c, u):
             nc.vector.tensor_copy(
@@ -125,48 +121,47 @@ def tile_moe_shr_lin_silu_kernel(tc, xT, w, b, gate, offs, out):
                 pairs[c][:].bitcast(dt).rearrange("p (u t) -> p t u", u=2)[:, h * H:(h + 1) * H],
             )
 
-        def weave_r():
+        def weave_r(c):
             nc.vector.tensor_copy(
-                woven_r[:].bitcast(F32).rearrange("p (t i u) -> p t u i", i=2, u=2),
+                woven_r[c % 2][:].bitcast(F32).rearrange("p (t i u) -> p t u i", i=2, u=2),
                 gathered[:].bitcast(F32).rearrange("p (u t i) -> p t u i", i=2, u=2),
             )
 
         def quant_r(c):
-            nc.vector.quantize_mx(out=xr_codes[c][:].bitcast(FP8X4), scales=xr_scales[c][:], in_=woven_r[:])
+            nc.vector.quantize_mx(out=xr_codes[c][:].bitcast(FP8X4), scales=xr_scales[c][:], in_=woven_r[c % 2][:])
 
         def quant_s(c, h=None):
             s = slice(0, T) if h is None else slice(h * H, (h + 1) * H)
-            nc.vector.quantize_mx(out=xs_codes[c][:, s].bitcast(FP8X4), scales=xs_scales[c][:, s],
+            nc.vector.quantize_mx(out=xs_codes[c][:, s].bitcast(FP8X4), scales=shared_scales(c, s),
                                   in_=woven_s[:] if h is None else staged(c, h))
 
-        def routed(e, c):
-            q = block(e, c)
+        def multiply(acc, e, c, codes, scales):
+            q = slice((PASSES * e + c) * N, (PASSES * e + c + 1) * N)
+            nc.tensor.matmul_mx(
+                out=acc, lhsT=w_codes[:, q].bitcast(FP8X4), lhsT_scale=w_scales[:, q],
+                rhs=codes.bitcast(FP8X4), rhs_scale=scales,
+                start=(c == 0), stop=(c == last),
+            )
+
+        def routed(e):
             s = slice(e * C, (e + 1) * C)
-            nc.tensor.matmul_mx(
-                out=acc_r[e][:], lhsT=w_codes[:, q].bitcast(FP8X4), lhsT_scale=w_scales[:, q],
-                rhs=xr_codes[c][:, s].bitcast(FP8X4), rhs_scale=xr_scales[c][:, s],
-                start=(c == 0), stop=(c == PASSES - 1),
-            )
+            for c in range(PASSES):
+                multiply(acc_r[e][:], e, c, xr_codes[c][:, s], xr_scales[c][:, s])
 
-        def shared(c, h):
-            q = block(E, c)
-            s = slice(h * H, (h + 1) * H)
-            nc.tensor.matmul_mx(
-                out=acc_s[h][:], lhsT=w_codes[:, q].bitcast(FP8X4), lhsT_scale=w_scales[:, q],
-                rhs=xs_codes[c][:, s].bitcast(FP8X4), rhs_scale=xs_scales[c][:, s],
-                start=(c == 0), stop=(c == PASSES - 1),
-            )
+        def shared(c0):
+            for h in range(2):
+                s = slice(h * H, (h + 1) * H)
+                for c in range(c0, c0 + 2):
+                    multiply(acc_s[h][:], E, c, xs_codes[c][:, s], shared_scales(c, s))
 
-        y = w_shared[:, 1024 - C:1024 + C]
         ys = keep.tile([P, T], F32, name="ys")
         res = keep.tile([P, T], F32, name="res")
 
-        def act_r(e):
-            s = slice(e * C, (e + 1) * C)
-            nc.scalar.activation(y[:, s], acc_r[e][:], SILU, bias=bias[:, e:e + 1])
+        def act_r(y, e, lo, hi):
+            nc.scalar.activation(y, acc_r[e][:, lo:hi], SILU, bias=bias[:, e:e + 1])
 
-        def scatter(lo, hi):
-            nc.vector.tensor_tensor(scattered[:].indirect(offsets[:, lo // 16:hi // 16]), y[:, lo:hi], gates[:, lo:hi], MULT)
+        def scatter(y, lo, hi):
+            nc.vector.tensor_tensor(scattered[:].indirect(offsets[:, lo // 16:hi // 16]), y, gates[:, lo:hi], MULT)
 
         def act_s(h):
             nc.scalar.activation(ys[:, h * H:(h + 1) * H], acc_s[h][:], SILU, bias=bias[:, E:E + 1])
@@ -177,13 +172,7 @@ def tile_moe_shr_lin_silu_kernel(tc, xT, w, b, gate, offs, out):
             nc.sync.dma_start(out=out[:, s], in_=res[:, s])
 
         cs, cv, cg = nc.scalar.copy, nc.vector.tensor_copy, nc.gpsimd.tensor_copy
-        last = PASSES - 1
         for c in range(PASSES):
-            if c == last:
-                round_w(0)
-                quant_w(0)
-                for e in range(E):
-                    routed(e, 0)
             round_x(c, 0, 0)
             round_x(c, 0, 1, cv if c == 0 else cs)
             if c == 0:
@@ -197,34 +186,36 @@ def tile_moe_shr_lin_silu_kernel(tc, xT, w, b, gate, offs, out):
             round_x(c, 1, 1)
             gather(c, 1)
             weave_s(c, 1, cg, U32)
-            weave_r()
+            if c > 1:
+                quant_r(c - 1)
+            weave_r(c)
             if c < last:
                 quant_s(c, 1 if c == 0 else None)
+            if c == 0:
                 quant_r(c)
+        round_w(0)
         round_w(1)
-        round_w(2)
-        quant_w(1, 2)
+        quant_w(0, 2)
         quant_r(last)
+        routed(0)
+        quant_s(last, 0)
+        round_w(2)
         round_w(3)
-        quant_w(3)
-        for c in range(1, PASSES):
-            for e in range(E):
-                routed(e, c)
-        quant_s(last)
+        quant_w(2, 2)
+        routed(1)
+        quant_s(last, 1)
         round_w(4)
-        act_r(0)
         quant_w(4)
-        for h in range(2):
-            for c in range(2):
-                shared(c, h)
-        scatter(0, 192)
+        shared(0)
+        y_first = w_raw[4][:, :C]
+        act_r(y_first, 0, 0, C)
+        scatter(y_first, 0, C)
         round_w(5)
-        act_r(1)
         quant_w(5)
-        for h in range(2):
-            for c in range(2, PASSES):
-                shared(c, h)
-        scatter(192, S)
+        shared(2)
+        y_second = w_raw[5][:, :C]
+        act_r(y_second, 1, 0, C)
+        scatter(y_second, C, S)
         for h in range(2):
             act_s(h)
         for h in range(2):

@@ -78,7 +78,7 @@ def tile_moe_shr_lin_silu_kernel(tc, xT, w, b, gate, offs, out):
             return xs_scales[c][:, s] if c < last else xs_scales_last[s.start // H][:]
 
         xr_codes = [keep.tile([P, S], U32, name="xr_codes_%d" % c, align_bytes=64,
-                              tag="x_raw_%d_1_1" % (c + 1) if c > 0 else "xr_codes_0") for c in range(last)]
+                              tag="x_raw_%d_0_1" % (c + 1)) for c in range(last)]
         xr_codes.append(reuse.tile([P, S], U32, name="xr_codes_last", align_bytes=64, offset=4096))
         xr_scales = [keep.tile([P, S], U8, name="xr_scales_%d" % c, align_bytes=64) for c in range(PASSES)]
         w_bf = keep.tile([P, 12 * 512], BF16, name="w_bf", align_bytes=64)
@@ -87,7 +87,7 @@ def tile_moe_shr_lin_silu_kernel(tc, xT, w, b, gate, offs, out):
         pairs = [keep.tile([P, 4 * T], BF16, name="pairs_%d" % c, align_bytes=64) for c in range(PASSES)]
         woven_s = keep.tile([P, 4 * T], BF16, name="woven_s", align_bytes=64)
         gathered = keep.tile([P, 4 * S], BF16, name="gathered", align_bytes=64)
-        woven_r = [keep.tile([P, 4 * S], BF16, name="woven_r_%d" % c, align_bytes=64) for c in range(2)]
+        woven_r = keep.tile([P, 4 * S], BF16, name="woven_r", align_bytes=64)
 
         def round_x(c, h, u, copy=nc.scalar.copy):
             run = 1 if c == 0 else 4
@@ -123,12 +123,12 @@ def tile_moe_shr_lin_silu_kernel(tc, xT, w, b, gate, offs, out):
 
         def weave_r(c):
             nc.vector.tensor_copy(
-                woven_r[c % 2][:].bitcast(F32).rearrange("p (t i u) -> p t u i", i=2, u=2),
+                woven_r[:].bitcast(F32).rearrange("p (t i u) -> p t u i", i=2, u=2),
                 gathered[:].bitcast(F32).rearrange("p (u t i) -> p t u i", i=2, u=2),
             )
 
         def quant_r(c):
-            nc.vector.quantize_mx(out=xr_codes[c][:].bitcast(FP8X4), scales=xr_scales[c][:], in_=woven_r[c % 2][:])
+            nc.vector.quantize_mx(out=xr_codes[c][:].bitcast(FP8X4), scales=xr_scales[c][:], in_=woven_r[:])
 
         def quant_s(c, h=None):
             s = slice(0, T) if h is None else slice(h * H, (h + 1) * H)
@@ -173,9 +173,9 @@ def tile_moe_shr_lin_silu_kernel(tc, xT, w, b, gate, offs, out):
 
         cs, cv, cg = nc.scalar.copy, nc.vector.tensor_copy, nc.gpsimd.tensor_copy
         for c in range(PASSES):
-            round_x(c, 0, 0)
-            round_x(c, 0, 1, cv if c == 0 else cs)
             if c == 0:
+                round_x(c, 0, 0)
+                round_x(c, 0, 1, cv)
                 weave_s(c, 0, cv, F32)
             round_x(c, 1, 0)
             if c == 0:
@@ -186,12 +186,12 @@ def tile_moe_shr_lin_silu_kernel(tc, xT, w, b, gate, offs, out):
             round_x(c, 1, 1)
             gather(c, 1)
             weave_s(c, 1, cg, U32)
-            if c > 1:
-                quant_r(c - 1)
             weave_r(c)
             if c < last:
                 quant_s(c, 1 if c == 0 else None)
-            if c == 0:
+            if c < last:
+                round_x(c + 1, 0, 0)
+                round_x(c + 1, 0, 1)
                 quant_r(c)
         round_w(0)
         round_w(1)

@@ -39,7 +39,7 @@ def tile_moe_shr_lin_silu_kernel(tc, xT, w, b, gate, offs, out):
         nc.scalar.activation(warm[:], warm[:], SILU)
         nc.gpsimd.memset(scattered[:], 0.0)
 
-        x_raw = [[[keep.tile([P, 2 * H], F32, name="x_raw_%d_%d_%d" % (c, h, u), tag="x_raw_%d_%d_%d" % (c, h, u), align_bytes=64) for u in range(2)]
+        x_raw = [[[keep.tile([P, 2 * H], F32, name="x_raw_%d_%d_%d" % (c, h, u)) for u in range(2)]
                   for h in range(2)] for c in range(PASSES)]
         w_raw = [reuse.tile([P, 1024], F32, name="w_raw_%d" % i, align_bytes=64, offset=4096 * i) for i in range(6)]
 
@@ -77,8 +77,7 @@ def tile_moe_shr_lin_silu_kernel(tc, xT, w, b, gate, offs, out):
         def shared_scales(c, s):
             return xs_scales[c][:, s] if c < last else xs_scales_last[s.start // H][:]
 
-        xr_codes = [keep.tile([P, S], U32, name="xr_codes_%d" % c, align_bytes=64,
-                              tag="x_raw_%d_0_1" % (c + 1)) for c in range(last)]
+        xr_codes = [keep.tile([P, S], U32, name="xr_codes_%d" % c, align_bytes=64) for c in range(last)]
         xr_codes.append(reuse.tile([P, S], U32, name="xr_codes_last", align_bytes=64, offset=4096))
         xr_scales = [keep.tile([P, S], U8, name="xr_scales_%d" % c, align_bytes=64) for c in range(PASSES)]
         w_bf = keep.tile([P, 12 * 512], BF16, name="w_bf", align_bytes=64)
@@ -173,9 +172,9 @@ def tile_moe_shr_lin_silu_kernel(tc, xT, w, b, gate, offs, out):
 
         cs, cv, cg = nc.scalar.copy, nc.vector.tensor_copy, nc.gpsimd.tensor_copy
         for c in range(PASSES):
+            round_x(c, 0, 0)
+            round_x(c, 0, 1, cv if c == 0 else cs)
             if c == 0:
-                round_x(c, 0, 0)
-                round_x(c, 0, 1, cv)
                 weave_s(c, 0, cv, F32)
             round_x(c, 1, 0)
             if c == 0:
@@ -189,9 +188,6 @@ def tile_moe_shr_lin_silu_kernel(tc, xT, w, b, gate, offs, out):
             weave_r(c)
             if c < last:
                 quant_s(c, 1 if c == 0 else None)
-            if c < last:
-                round_x(c + 1, 0, 0)
-                round_x(c + 1, 0, 1)
                 quant_r(c)
         round_w(0)
         round_w(1)

@@ -165,8 +165,8 @@ def tile_moe_shr_lin_silu_kernel(tc, xT, w, b, gate, offs, out):
         def act_s(h):
             nc.scalar.activation(ys[:, h * H:(h + 1) * H], acc_s[h][:], SILU, bias=bias[:, E:E + 1])
 
-        def finish(h):
-            s = slice(h * H, (h + 1) * H)
+        def finish(lo, hi):
+            s = slice(lo, hi)
             nc.vector.tensor_tensor(res[:, s], ys[:, s], scattered[:, s], ADD)
             nc.sync.dma_start(out=out[:, s], in_=res[:, s])
 
@@ -214,5 +214,6 @@ def tile_moe_shr_lin_silu_kernel(tc, xT, w, b, gate, offs, out):
         scatter(y_second, C, S)
         for h in range(2):
             act_s(h)
-        for h in range(2):
-            finish(h)
+        cuts = (0, N, H, T - N, T)
+        for lo, hi in zip(cuts, cuts[1:]):
+            finish(lo, hi)

@@ -34,18 +34,17 @@ def tile_moe_shr_lin_silu_kernel(tc, xT, w, b, gate, offs, out):
         scattered = keep.tile([P, T], F32, name="scattered")
         warm = keep.tile([P, 1], F32, name="warm")
 
-        nc.scalar.dma_start(out=bias[:], in_=b)
         nc.gpsimd.memset(warm[:], 0.0)
         nc.scalar.activation(warm[:], warm[:], SILU)
         nc.gpsimd.memset(scattered[:], 0.0)
 
-        x_raw = [[[keep.tile([P, 2 * H], F32, name="x_raw_%d_%d_%d" % (c, h, u)) for u in range(2)]
+        x_raw = [[[keep.tile([P, 2 * H], F32, name="x_raw_%d_%d_%d" % (c, h, u))[:] for u in range(2)]
                   for h in range(2)] for c in range(PASSES)]
         w_raw = [reuse.tile([P, 1024], F32, name="w_raw_%d" % i, align_bytes=64, offset=4096 * i) for i in range(6)]
 
         def load_x(c, h, u):
             rows = xT[c * 512:(c + 1) * 512, :].rearrange("(p j) t -> p j t", j=4)
-            nc.sync.dma_start(out=x_raw[c][h][u][:].rearrange("p (j t) -> p j t", j=2),
+            nc.sync.dma_start(out=x_raw[c][h][u].rearrange("p (j t) -> p j t", j=2),
                               in_=rows[:, 2 * u:2 * u + 2, h * H:(h + 1) * H])
 
         def load_w(i):
@@ -64,6 +63,8 @@ def tile_moe_shr_lin_silu_kernel(tc, xT, w, b, gate, offs, out):
                     load_x(c, h, u)
         for i in range(5):
             load_w(i)
+            if i == 2:
+                nc.sync.dma_start(out=bias[:], in_=b)
         nc.sync.dma_start(out=gates[:], in_=gate)
         load_w(5)
 
@@ -90,7 +91,7 @@ def tile_moe_shr_lin_silu_kernel(tc, xT, w, b, gate, offs, out):
 
         def round_x(c, h, u, copy=nc.scalar.copy):
             run = 1 if c == 0 else 4
-            src = x_raw[c][h][u][:].rearrange("p (j t i) -> p t j i", j=2, i=run)
+            src = x_raw[c][h][u].rearrange("p (j t i) -> p t j i", j=2, i=run)
             lo = u * 2 * T + h * 2 * H
             copy(pairs[c][:, lo:lo + 2 * H].rearrange("p (t i j) -> p t j i", j=2, i=run), src)
 
@@ -162,8 +163,8 @@ def tile_moe_shr_lin_silu_kernel(tc, xT, w, b, gate, offs, out):
         def scatter(y, lo, hi):
             nc.vector.tensor_tensor(scattered[:].indirect(offsets[:, lo // 16:hi // 16]), y, gates[:, lo:hi], MULT)
 
-        def act_s(h):
-            nc.scalar.activation(ys[:, h * H:(h + 1) * H], acc_s[h][:], SILU, bias=bias[:, E:E + 1])
+        def act_s(lo, hi):
+            nc.scalar.activation(ys[:, lo:hi], acc_s[lo // H][:, lo % H:lo % H + hi - lo], SILU, bias=bias[:, E:E + 1])
 
         def finish(lo, hi):
             s = slice(lo, hi)
@@ -212,8 +213,7 @@ def tile_moe_shr_lin_silu_kernel(tc, xT, w, b, gate, offs, out):
         y_second = w_raw[5][:, :C]
         act_r(y_second, 1, 0, C)
         scatter(y_second, C, S)
-        for h in range(2):
-            act_s(h)
-        cuts = (0, N, H, T - N, T)
+        cuts = range(0, T + 1, T // 4)
         for lo, hi in zip(cuts, cuts[1:]):
+            act_s(lo, hi)
             finish(lo, hi)

from contextlib import ExitStack

import concourse.mybir as mybir

K, T, E, C, N = 2048, 1024, 2, 256, 128
S = E * C
P = 128
PASSES = K // 512
H = T // 2
FLOPS = 2 * K * N * (T + S)

F32 = mybir.dt.float32
BF16 = mybir.dt.bfloat16
U32 = mybir.dt.uint32
U16 = mybir.dt.uint16
U8 = mybir.dt.uint8
FP8X4 = mybir.dt.float8_e4m3fn_x4
SILU = mybir.ActivationFunctionType.Silu
MULT = mybir.AluOpType.mult
ADD = mybir.AluOpType.add


def tile_moe_shr_lin_silu_kernel(tc, xT, w, b, gate, offs, out):
    nc = tc.nc
    last = PASSES - 1
    with ExitStack() as ctx:
        keep = ctx.enter_context(tc.tile_pool(name="keep", bufs=1))
        reuse = ctx.enter_context(tc.tile_pool(name="reuse", bufs=1))
        psum = ctx.enter_context(tc.psum_pool(name="psum", bufs=1))

        offsets = keep.tile([P, S // 16], U16, name="offsets")
        bias = keep.tile([P, E + 1], F32, name="bias")
        gates = keep.tile([P, S], F32, name="gates")
        scattered = keep.tile([P, T], F32, name="scattered")
        warm = keep.tile([P, 1], F32, name="warm")

        nc.gpsimd.memset(warm[:], 0.0)
        nc.scalar.activation(warm[:], warm[:], SILU)
        nc.gpsimd.memset(scattered[:], 0.0)

        x_raw = [[[keep.tile([P, 2 * H], F32, name="x_raw_%d_%d_%d" % (c, h, u))[:] for u in range(2)]
                  for h in range(2)] for c in range(PASSES)]
        w_raw = [reuse.tile([P, 1024], F32, name="w_raw_%d" % i, align_bytes=64, offset=4096 * i) for i in range(6)]

        def load_x(c, h, u):
            rows = xT[c * 512:(c + 1) * 512, :].rearrange("(p j) t -> p j t", j=4)
            nc.sync.dma_start(out=x_raw[c][h][u].rearrange("p (j t) -> p j t", j=2),
                              in_=rows[:, 2 * u:2 * u + 2, h * H:(h + 1) * H])

        def load_w(i):
            e, k0 = i // 2, (i % 2) * 1024
            nc.sync.dma_start(out=w_raw[i][:].rearrange("p (q r) -> p q r", q=2),
                              in_=w[e, k0:k0 + 1024, :].rearrange("(c p j) n -> p c (j n)", p=P, j=4))

        load_x(0, 0, 0)
        load_x(0, 0, 1)
        nc.sync.dma_start(offsets[:], offs)
        load_x(0, 1, 0)
        load_x(0, 1, 1)
        for c in range(1, PASSES):
            for h in range(2):
                for u in range(2):
                    load_x(c, h, u)
        for i in range(5):
            load_w(i)
            if i == 2:
                nc.sync.dma_start(out=bias[:], in_=b)
        nc.sync.dma_start(out=gates[:], in_=gate)
        load_w(5)

        acc_r = [psum.tile([P, C], F32, name="acc_r_%d" % e) for e in range(E)]
        acc_s = [psum.tile([P, 512], F32, name="acc_s_%d" % h) for h in range(2)]
        xs_codes = [keep.tile([P, T], U32, name="xs_codes_%d" % c, align_bytes=64) for c in range(PASSES)]
        xs_scales = [keep.tile([P, T], U8, name="xs_scales_%d" % c, align_bytes=64) for c in range(last)]
        xs_scales_last = [reuse.tile([P, H], U8, name="xs_scales_last_%d" % h, align_bytes=64, offset=(4096 + 2048, 3 * 4096)[h])
                          for h in range(2)]

        def shared_scales(c, s):
            return xs_scales[c][:, s] if c < last else xs_scales_last[s.start // H][:]

        xr_codes = [keep.tile([P, S], U32, name="xr_codes_%d" % c, align_bytes=64) for c in range(last)]
        xr_codes.append(reuse.tile([P, S], U32, name="xr_codes_last", align_bytes=64, offset=4096))
        xr_scales = [keep.tile([P, S], U8, name="xr_scales_%d" % c, align_bytes=64) for c in range(PASSES)]
        w_bf = keep.tile([P, 12 * 512], BF16, name="w_bf", align_bytes=64)
        w_codes = keep.tile([P, 12 * N], U32, name="w_codes", align_bytes=64)
        w_scales = keep.tile([P, 12 * N], U8, name="w_scales", align_bytes=64)
        pairs = [keep.tile([P, 4 * T], BF16, name="pairs_%d" % c, align_bytes=64) for c in range(PASSES)]
        woven_s = keep.tile([P, 4 * T], BF16, name="woven_s", align_bytes=64)
        gathered = keep.tile([P, 4 * S], BF16, name="gathered", align_bytes=64)
        woven_r = keep.tile([P, 4 * S], BF16, name="woven_r", align_bytes=64)

        def round_x(c, h, u, copy=nc.scalar.copy):
            run = 1 if c == 0 else 4
            src = x_raw[c][h][u].rearrange("p (j t i) -> p t j i", j=2, i=run)
            lo = u * 2 * T + h * 2 * H
            copy(pairs[c][:, lo:lo + 2 * H].rearrange("p (t i j) -> p t j i", j=2, i=run), src)

        def round_w(i):
            nc.scalar.copy(
                w_bf[:, i * 1024:(i + 1) * 1024].rearrange("p (q c i j) -> p q c j i", q=2, i=4, j=4),
                w_raw[i][:].rearrange("p (q j c i) -> p q c j i", q=2, i=4, j=4),
            )

        def quant_w(i, n=1):
            s = slice(i * 2 * N, (i + n) * 2 * N)
            nc.vector.quantize_mx(out=w_codes[:, s].bitcast(FP8X4), scales=w_scales[:, s], in_=w_bf[:, i * 1024:(i + n) * 1024])

        def gather(c, u):
            nc.vector.tensor_copy(
                gathered[:, u * 2 * S:(u + 1) * 2 * S].bitcast(U32),
                pairs[c][:, u * 2 * T:(u + 1) * 2 * T].bitcast(U32).indirect(offsets[:]),
            )

        def staged(c, h):
            h = 1 - h if c == 0 else h
            return woven_s[:, 4 * h * H:4 * (h + 1) * H]

        def weave_s(c, h, copy, dt):
            copy(
                staged(c, h).bitcast(dt).rearrange("p (t u) -> p t u", u=2),
                pairs[c][:].bitcast(dt).rearrange("p (u t) -> p t u", u=2)[:, h * H:(h + 1) * H],
            )

        def weave_r(c):
            nc.vector.tensor_copy(
                woven_r[:].bitcast(F32).rearrange("p (t i u) -> p t u i", i=2, u=2),
                gathered[:].bitcast(F32).rearrange("p (u t i) -> p t u i", i=2, u=2),
            )

        def quant_r(c):
            nc.vector.quantize_mx(out=xr_codes[c][:].bitcast(FP8X4), scales=xr_scales[c][:], in_=woven_r[:])

        def quant_s(c, h=None):
            s = slice(0, T) if h is None else slice(h * H, (h + 1) * H)
            nc.vector.quantize_mx(out=xs_codes[c][:, s].bitcast(FP8X4), scales=shared_scales(c, s),
                                  in_=woven_s[:] if h is None else staged(c, h))

        def multiply(acc, e, c, codes, scales):
            q = slice((PASSES * e + c) * N, (PASSES * e + c + 1) * N)
            nc.tensor.matmul_mx(
                out=acc, lhsT=w_codes[:, q].bitcast(FP8X4), lhsT_scale=w_scales[:, q],
                rhs=codes.bitcast(FP8X4), rhs_scale=scales,
                start=(c == 0), stop=(c == last),
            )

        def routed(e):
            s = slice(e * C, (e + 1) * C)
            for c in range(PASSES):
                multiply(acc_r[e][:], e, c, xr_codes[c][:, s], xr_scales[c][:, s])

        def shared(c0):
            for h in range(2):
                s = slice(h * H, (h + 1) * H)
                for c in range(c0, c0 + 2):
                    multiply(acc_s[h][:], E, c, xs_codes[c][:, s], shared_scales(c, s))

        ys = keep.tile([P, T], F32, name="ys")
        res = keep.tile([P, T], F32, name="res")

        def act_r(y, e, lo, hi):
            nc.scalar.activation(y, acc_r[e][:, lo:hi], SILU, bias=bias[:, e:e + 1])

        def scatter(y, lo, hi):
            nc.vector.tensor_tensor(scattered[:].indirect(offsets[:, lo // 16:hi // 16]), y, gates[:, lo:hi], MULT)

        def act_s(lo, hi):
            nc.scalar.activation(ys[:, lo:hi], acc_s[lo // H][:, lo % H:lo % H + hi - lo], SILU, bias=bias[:, E:E + 1])

        def finish(lo, hi):
            s = slice(lo, hi)
            nc.vector.tensor_tensor(res[:, s], ys[:, s], scattered[:, s], ADD)
            nc.sync.dma_start(out=out[:, s], in_=res[:, s])

        cs, cv, cg = nc.scalar.copy, nc.vector.tensor_copy, nc.gpsimd.tensor_copy
        for c in range(PASSES):
            round_x(c, 0, 0)
            round_x(c, 0, 1, cv if c == 0 else cs)
            if c == 0:
                weave_s(c, 0, cv, F32)
            round_x(c, 1, 0)
            if c == 0:
                quant_s(c, 0)
            gather(c, 0)
            if c > 0:
                weave_s(c, 0, cg, U32)
            round_x(c, 1, 1)
            gather(c, 1)
            weave_s(c, 1, cg, U32)
            weave_r(c)
            if c < last:
                quant_s(c, 1 if c == 0 else None)
                quant_r(c)
        round_w(0)
        round_w(1)
        quant_w(0, 2)
        quant_r(last)
        routed(0)
        quant_s(last, 0)
        round_w(2)
        round_w(3)
        quant_w(2, 2)
        routed(1)
        quant_s(last, 1)
        round_w(4)
        quant_w(4)
        shared(0)
        y_first = w_raw[4][:, :C]
        act_r(y_first, 0, 0, C)
        scatter(y_first, 0, C)
        round_w(5)
        quant_w(5)
        shared(2)
        y_second = w_raw[5][:, :C]
        act_r(y_second, 1, 0, C)
        scatter(y_second, C, S)
        cuts = range(0, T + 1, T // 4)
        for lo, hi in zip(cuts, cuts[1:]):
            act_s(lo, hi)
            finish(lo, hi)
